import numpy as np
import ml_dtypes


def mxq(x, axis, fmt="e4m3"):
    dtype, down = {"e4m3": (ml_dtypes.float8_e4m3fn, 7), "e5m2": (ml_dtypes.float8_e5m2, 14)}[fmt]
    v = np.moveaxis(np.asarray(x, np.float32).astype(ml_dtypes.bfloat16).astype(np.float64), axis, -1)
    blocks = v.reshape(v.shape[:-1] + (-1, 32))
    amax = np.abs(blocks).max(-1, keepdims=True)
    byte = np.maximum(np.where(amax > 0, np.frexp(amax)[1] - 1 + 127, 0) - down, 1)
    scale = np.exp2(byte - 127.0)
    codes = (blocks / scale).astype(np.float32).astype(dtype).astype(np.float64)
    return np.moveaxis((codes * scale).reshape(v.shape), -1, axis)


WIDE = False


def mx_kscale(k):
    if not WIDE:
        return np.ones(k)
    levels = np.array([10, -10, 5, -5, 0])
    if k % 512:
        return np.exp2(np.random.permutation(np.resize(levels, k // 32))).repeat(32)
    a = np.empty((k // 512, 16))
    for p in range(k // 512):
        a[p, :8] = np.random.permutation(np.resize(levels, 8))
        for g in range(8):
            far = levels[np.abs(levels - a[p, g]) >= 10]
            a[p, g + 8] = far[np.random.randint(len(far))]
    return np.exp2(a.ravel()).repeat(32)


def f64(x):
    return np.asarray(x).astype(np.float64)


def striped(idx):
    return np.tile(idx.reshape(-1, 16).T, (8, 1)).astype(np.uint16)


def unstriped(offs):
    return offs[:16].T.reshape(-1).astype(np.int64)


K, T, D, S, V, N = 512, 4096, 2, 1024, 512, 256


def setup_inputs():
    n = np.random.standard_normal
    s = mx_kscale(K)[:, None]
    return {
        "xT": (n((K, T)) * s).astype(np.float32),
        "w": (n((D, K, N)) / np.sqrt(K) / s[None]).astype(np.float32),
        "offs": striped(np.random.permutation(T)[:S]),
    }


def reference(xT, w, offs):
    idx = unstriped(offs)
    xq = mxq(f64(xT)[:, idx], 0, "e4m3")
    wq = mxq(f64(w), 1, "e4m3")
    y0 = wq[0].T @ xq[:, :V]
    y1 = wq[1].T @ xq[:, V:]
    return y0 * y1

@@ -1,0 +1,134 @@
+import concourse.mybir as mybir
+from concourse.masks import make_identity
+
+K, T, S, V, N = 512, 4096, 1024, 512, 256
+P = 128
+PACK = 4
+M_TILES = N // P
+PIECE = 256
+PIECES = V // PIECE
+
+FLOPS = 2 * K * N * S
+
+F32 = mybir.dt.float32
+BF16 = mybir.dt.bfloat16
+U32 = mybir.dt.uint32
+U16 = mybir.dt.uint16
+U8 = mybir.dt.uint8
+FP8X4 = mybir.dt.float8_e4m3fn_x4
+MULT = mybir.AluOpType.mult
+
+
+def tile_picked_pair_lin_mul_sub_e_kernel(tc, xT, w, offs, out):
+    nc = tc.nc
+    with (
+        tc.tile_pool(name="keep", bufs=1) as keep,
+        tc.psum_pool(name="psum", bufs=1) as psum,
+    ):
+        offsets = keep.tile([P, S // 16], U16, name="offsets")
+        nc.sync.dma_start(offsets[:], offs)
+
+        w_raw = [keep.tile([P, PACK, N], F32, name=f"w_raw{d}") for d in range(2)]
+        planes = [keep.tile([P, T], F32, name=f"plane{j}") for j in range(PACK)]
+        x_rows = xT.rearrange("(p j) t -> p j t", j=PACK)
+        nc.sync.dma_start(out=w_raw[0][:], in_=w[0].rearrange("(p j) n -> p j n", j=PACK))
+        for j in range(PACK):
+            nc.sync.dma_start(out=planes[j][:], in_=x_rows[:, j, :])
+        nc.sync.dma_start(out=w_raw[1][:], in_=w[1].rearrange("(p j) n -> p j n", j=PACK))
+
+        identity = keep.tile([P, P], F32, name="identity")
+        make_identity(nc, identity[:])
+
+        w_grouped = [[keep.tile([P, P, PACK], BF16, name=f"w_grouped{d}_{m}", align_bytes=64) for m in range(M_TILES)] for d in range(2)]
+        w_codes = [[keep.tile([P, P], U32, name=f"w_codes{d}_{m}", align_bytes=64) for m in range(M_TILES)] for d in range(2)]
+        w_scales = [[keep.tile([P, P], U8, name=f"w_scales{d}_{m}", align_bytes=64) for m in range(M_TILES)] for d in range(2)]
+        gathered = [[keep.tile([P, 2, V], F32, name=f"gathered{d}_{u}") for u in range(2)] for d in range(2)]
+        x_grouped = [[keep.tile([P, PIECE, PACK], BF16, name=f"x_grouped{d}_{i}", align_bytes=64) for i in range(PIECES)] for d in range(2)]
+        x_codes = [[keep.tile([P, PIECE], U32, name=f"x_codes{d}_{i}", align_bytes=64) for i in range(PIECES)] for d in range(2)]
+        x_scales = [[keep.tile([P, PIECE], U8, name=f"x_scales{d}_{i}", align_bytes=64) for i in range(PIECES)] for d in range(2)]
+        pieces = [slice(i * PIECE, (i + 1) * PIECE) for i in range(PIECES)]
+
+        def interleave_w(d, m):
+            nc.scalar.copy(
+                out=w_grouped[d][m][:],
+                in_=w_raw[d][:, :, m * P : (m + 1) * P].rearrange("p j n -> p n j"),
+            )
+
+        def quantise_w(d, m):
+            nc.vector.quantize_mx(
+                out=w_codes[d][m][:].bitcast(FP8X4),
+                scales=w_scales[d][m][:],
+                in_=w_grouped[d][m][:].rearrange("p n j -> p (n j)"),
+            )
+
+        def gather(j, d):
+            picked = planes[j][:].indirect(offsets[:, d * (V // 16) : (d + 1) * (V // 16)])
+            nc.vector.tensor_copy(gathered[d][j // 2][:, j % 2, :], picked)
+
+        def interleave_x(copy, d, i, u):
+            copy(
+                out=x_grouped[d][i][:, :, 2 * u : 2 * u + 2],
+                in_=gathered[d][u][:, :, pieces[i]].rearrange("p e v -> p v e"),
+            )
+
+        def quantise_x(d, i):
+            nc.vector.quantize_mx(
+                out=x_codes[d][i][:].bitcast(FP8X4),
+                scales=x_scales[d][i][:],
+                in_=x_grouped[d][i][:].rearrange("p v j -> p (v j)"),
+            )
+
+        def product(d, i, m, acc):
+            nc.tensor.matmul_mx(
+                out=acc,
+                lhsT=w_codes[d][m][:].bitcast(FP8X4),
+                lhsT_scale=w_scales[d][m][:],
+                rhs=x_codes[d][i][:].bitcast(FP8X4),
+                rhs_scale=x_scales[d][i][:],
+                start=True,
+                stop=True,
+            )
+
+        for m in range(M_TILES):
+            interleave_w(0, m)
+        for m in range(M_TILES):
+            quantise_w(0, m)
+        for j in range(PACK):
+            for d in range(2):
+                gather(j, d)
+            if j == 1:
+                for d in range(2):
+                    for i in range(PIECES):
+                        interleave_x(nc.scalar.copy, d, i, 0)
+
+        warm = psum.tile([P, 4, P], F32, name="warm", tag="spare")
+        for i in range(12):
+            nc.tensor.transpose(warm[:, i % 4, :], planes[PACK - 1][:, i * P : (i + 1) * P], identity[:])
+
+        for i in range(PIECES):
+            interleave_x(nc.scalar.copy, 0, i, 1)
+            interleave_x(nc.vector.tensor_copy, 1, i, 1)
+        for m in range(M_TILES):
+            interleave_w(1, m)
+
+        y0 = {}
+        for i in range(PIECES):
+            quantise_x(0, i)
+            for m in range(M_TILES):
+                bank = psum.tile([P, PIECE], F32, name=f"bank0_{i}_{m}")
+                product(0, i, m, bank[:])
+                y0[i, m] = keep.tile([P, PIECE], F32, name=f"y0_{i}_{m}")
+                nc.scalar.copy(out=y0[i, m][:], in_=bank[:])
+        quantise_x(1, 0)
+        quantise_w(1, 0)
+        quantise_x(1, 1)
+        quantise_w(1, 1)
+        for m in range(M_TILES):
+            for i in range(PIECES):
+                final = (m, i) == (M_TILES - 1, PIECES - 1)
+                bank = psum.tile([P, PIECE], F32, name=f"bank1_{i}_{m}", tag="spare" if final else f"bank1_{i}_{m}")
+                product(1, i, m, bank[:])
+                result = keep.tile([P, PIECE], F32, name=f"result{i}_{m}")
+                nc.vector.tensor_tensor(result[:], bank[:], y0[i, m][:], MULT)
+                queue = nc.sync if i else nc.scalar
+                queue.dma_start(out=out[m * P : (m + 1) * P, pieces[i]], in_=result[:])

@@ -1,5 +1,4 @@
 import concourse.mybir as mybir
-from concourse.masks import make_identity
 
 K, T, S, V, N = 512, 4096, 1024, 512, 256
 P = 128
@@ -7,6 +6,7 @@ PACK = 4
 M_TILES = N // P
 PIECE = 256
 PIECES = V // PIECE
+LAST_CHUNKS = (2048, 1024, 512, 512)
 
 FLOPS = 2 * K * N * S
 
@@ -17,6 +17,7 @@ U16 = mybir.dt.uint16
 U8 = mybir.dt.uint8
 FP8X4 = mybir.dt.float8_e4m3fn_x4
 MULT = mybir.AluOpType.mult
+COPY = mybir.ActivationFunctionType.Copy
 
 
 def tile_picked_pair_lin_mul_sub_e_kernel(tc, xT, w, offs, out):
@@ -27,23 +28,28 @@ def tile_picked_pair_lin_mul_sub_e_kernel(tc, xT, w, offs, out):
     ):
         offsets = keep.tile([P, S // 16], U16, name="offsets")
         nc.sync.dma_start(offsets[:], offs)
+        halves = [offsets[:, d * (V // 16) : (d + 1) * (V // 16)] for d in range(2)]
 
         w_raw = [keep.tile([P, PACK, N], F32, name=f"w_raw{d}") for d in range(2)]
         planes = [keep.tile([P, T], F32, name=f"plane{j}") for j in range(PACK)]
+        last = PACK - 1
+        last_bf16 = keep.tile([P, T], BF16, name="last_bf16")
+        starts = [sum(LAST_CHUNKS[:c]) for c in range(len(LAST_CHUNKS))]
+        chunks = [slice(a, a + n) for a, n in zip(starts, LAST_CHUNKS)]
         x_rows = xT.rearrange("(p j) t -> p j t", j=PACK)
         nc.sync.dma_start(out=w_raw[0][:], in_=w[0].rearrange("(p j) n -> p j n", j=PACK))
-        for j in range(PACK):
+        for j in range(last):
             nc.sync.dma_start(out=planes[j][:], in_=x_rows[:, j, :])
+        for chunk in chunks:
+            nc.sync.dma_start(out=planes[last][:, chunk], in_=x_rows[:, last, chunk])
         nc.sync.dma_start(out=w_raw[1][:], in_=w[1].rearrange("(p j) n -> p j n", j=PACK))
-
-        identity = keep.tile([P, P], F32, name="identity")
-        make_identity(nc, identity[:])
 
         w_grouped = [[keep.tile([P, P, PACK], BF16, name=f"w_grouped{d}_{m}", align_bytes=64) for m in range(M_TILES)] for d in range(2)]
         w_codes = [[keep.tile([P, P], U32, name=f"w_codes{d}_{m}", align_bytes=64) for m in range(M_TILES)] for d in range(2)]
         w_scales = [[keep.tile([P, P], U8, name=f"w_scales{d}_{m}", align_bytes=64) for m in range(M_TILES)] for d in range(2)]
-        gathered = [[keep.tile([P, 2, V], F32, name=f"gathered{d}_{u}") for u in range(2)] for d in range(2)]
-        x_grouped = [[keep.tile([P, PIECE, PACK], BF16, name=f"x_grouped{d}_{i}", align_bytes=64) for i in range(PIECES)] for d in range(2)]
+        staged_pair = keep.tile([P, 2, V], F32, name="staged_pair")
+        staged = keep.tile([P, V], F32, name="staged")
+        x_grouped = [keep.tile([P, V, PACK], BF16, name=f"x_grouped{d}", align_bytes=64) for d in range(2)]
         x_codes = [[keep.tile([P, PIECE], U32, name=f"x_codes{d}_{i}", align_bytes=64) for i in range(PIECES)] for d in range(2)]
         x_scales = [[keep.tile([P, PIECE], U8, name=f"x_scales{d}_{i}", align_bytes=64) for i in range(PIECES)] for d in range(2)]
         pieces = [slice(i * PIECE, (i + 1) * PIECE) for i in range(PIECES)]
@@ -62,25 +68,19 @@ def tile_picked_pair_lin_mul_sub_e_kernel(tc, xT, w, offs, out):
             )
 
         def gather(j, d):
-            picked = planes[j][:].indirect(offsets[:, d * (V // 16) : (d + 1) * (V // 16)])
-            nc.vector.tensor_copy(gathered[d][j // 2][:, j % 2, :], picked)
-
-        def interleave_x(copy, d, i, u):
-            copy(
-                out=x_grouped[d][i][:, :, 2 * u : 2 * u + 2],
-                in_=gathered[d][u][:, :, pieces[i]].rearrange("p e v -> p v e"),
-            )
+            nc.vector.tensor_copy(x_grouped[d][:, :, j], planes[j][:].indirect(halves[d]))
 
         def quantise_x(d, i):
             nc.vector.quantize_mx(
                 out=x_codes[d][i][:].bitcast(FP8X4),
                 scales=x_scales[d][i][:],
-                in_=x_grouped[d][i][:].rearrange("p v j -> p (v j)"),
+                in_=x_grouped[d][:, pieces[i], :].rearrange("p v j -> p (v j)"),
             )
 
-        def product(d, i, m, acc):
+        def product(d, i, m):
+            bank = psum.tile([P, PIECE], F32, name=f"bank{d}_{i}_{m}")
             nc.tensor.matmul_mx(
-                out=acc,
+                out=bank[:],
                 lhsT=w_codes[d][m][:].bitcast(FP8X4),
                 lhsT_scale=w_scales[d][m][:],
                 rhs=x_codes[d][i][:].bitcast(FP8X4),
@@ -88,47 +88,44 @@ def tile_picked_pair_lin_mul_sub_e_kernel(tc, xT, w, offs, out):
                 start=True,
                 stop=True,
             )
+            return bank
 
         for m in range(M_TILES):
             interleave_w(0, m)
         for m in range(M_TILES):
             quantise_w(0, m)
-        for j in range(PACK):
-            for d in range(2):
-                gather(j, d)
-            if j == 1:
-                for d in range(2):
-                    for i in range(PIECES):
-                        interleave_x(nc.scalar.copy, d, i, 0)
-
-        warm = psum.tile([P, 4, P], F32, name="warm", tag="spare")
-        for i in range(12):
-            nc.tensor.transpose(warm[:, i % 4, :], planes[PACK - 1][:, i * P : (i + 1) * P], identity[:])
-
-        for i in range(PIECES):
-            interleave_x(nc.scalar.copy, 0, i, 1)
-            interleave_x(nc.vector.tensor_copy, 1, i, 1)
+        for j in range(2):
+            nc.vector.tensor_copy(staged_pair[:, j, :], planes[j][:].indirect(halves[1]))
+            gather(j, 0)
+        nc.scalar.copy(out=x_grouped[1][:, :, 0:2], in_=staged_pair[:].rearrange("p e v -> p v e"))
+        nc.vector.tensor_copy(staged[:], planes[last - 1][:].indirect(halves[1]))
+        nc.scalar.copy(out=x_grouped[1][:, :, last - 1], in_=staged[:])
+        gather(last - 1, 0)
+        for c, chunk in enumerate(chunks):
+            cast = nc.scalar.copy if c % 2 else nc.vector.tensor_copy
+            cast(out=last_bf16[:, chunk], in_=planes[last][:, chunk])
+        gather(last, 0)
+        nc.scalar.activation(x_grouped[1][:, :, last], last_bf16[:].indirect(halves[1]), COPY)
         for m in range(M_TILES):
             interleave_w(1, m)
 
-        y0 = {}
+        banks0 = {}
         for i in range(PIECES):
             quantise_x(0, i)
             for m in range(M_TILES):
-                bank = psum.tile([P, PIECE], F32, name=f"bank0_{i}_{m}")
-                product(0, i, m, bank[:])
-                y0[i, m] = keep.tile([P, PIECE], F32, name=f"y0_{i}_{m}")
-                nc.scalar.copy(out=y0[i, m][:], in_=bank[:])
-        quantise_x(1, 0)
-        quantise_w(1, 0)
-        quantise_x(1, 1)
-        quantise_w(1, 1)
+                banks0[i, m] = product(0, i, m)
+        for i in range(PIECES):
+            quantise_x(1, i)
+        for m in range(M_TILES):
+            quantise_w(1, m)
+        y0 = {}
         for m in range(M_TILES):
             for i in range(PIECES):
-                final = (m, i) == (M_TILES - 1, PIECES - 1)
-                bank = psum.tile([P, PIECE], F32, name=f"bank1_{i}_{m}", tag="spare" if final else f"bank1_{i}_{m}")
-                product(1, i, m, bank[:])
+                y0[i, m] = keep.tile([P, PIECE], F32, name=f"y0_{i}_{m}")
+                nc.scalar.copy(out=y0[i, m][:], in_=banks0[i, m][:])
+        for m in range(M_TILES):
+            for i in range(PIECES):
+                bank = product(1, i, m)
                 result = keep.tile([P, PIECE], F32, name=f"result{i}_{m}")
                 nc.vector.tensor_tensor(result[:], bank[:], y0[i, m][:], MULT)
-                queue = nc.sync if i else nc.scalar
-                queue.dma_start(out=out[m * P : (m + 1) * P, pieces[i]], in_=result[:])
+                nc.sync.dma_start(out=out[m * P : (m + 1) * P, pieces[i]], in_=result[:])

@@ -3,9 +3,12 @@ import concourse.mybir as mybir
 K, T, S, V, N = 512, 4096, 1024, 512, 256
 P = 128
 PACK = 4
+RUN = 4
 M_TILES = N // P
 PIECE = 256
 PIECES = V // PIECE
+WIDTH = V + N
+FRONT = 512
 LAST_CHUNKS = (2048, 1024, 512, 512)
 
 FLOPS = 2 * K * N * S
@@ -37,95 +40,87 @@ def tile_picked_pair_lin_mul_sub_e_kernel(tc, xT, w, offs, out):
         starts = [sum(LAST_CHUNKS[:c]) for c in range(len(LAST_CHUNKS))]
         chunks = [slice(a, a + n) for a, n in zip(starts, LAST_CHUNKS)]
         x_rows = xT.rearrange("(p j) t -> p j t", j=PACK)
-        nc.sync.dma_start(out=w_raw[0][:], in_=w[0].rearrange("(p j) n -> p j n", j=PACK))
         for j in range(last):
             nc.sync.dma_start(out=planes[j][:], in_=x_rows[:, j, :])
         for chunk in chunks:
             nc.sync.dma_start(out=planes[last][:, chunk], in_=x_rows[:, last, chunk])
-        nc.sync.dma_start(out=w_raw[1][:], in_=w[1].rearrange("(p j) n -> p j n", j=PACK))
+        for d in range(2):
+            nc.sync.dma_start(out=w_raw[d][:], in_=w[d].rearrange("(p j) n -> p j n", j=PACK))
 
-        w_grouped = [[keep.tile([P, P, PACK], BF16, name=f"w_grouped{d}_{m}", align_bytes=64) for m in range(M_TILES)] for d in range(2)]
-        w_codes = [[keep.tile([P, P], U32, name=f"w_codes{d}_{m}", align_bytes=64) for m in range(M_TILES)] for d in range(2)]
-        w_scales = [[keep.tile([P, P], U8, name=f"w_scales{d}_{m}", align_bytes=64) for m in range(M_TILES)] for d in range(2)]
         staged_pair = keep.tile([P, 2, V], F32, name="staged_pair")
         staged = keep.tile([P, V], F32, name="staged")
-        x_grouped = [keep.tile([P, V, PACK], BF16, name=f"x_grouped{d}", align_bytes=64) for d in range(2)]
-        x_codes = [[keep.tile([P, PIECE], U32, name=f"x_codes{d}_{i}", align_bytes=64) for i in range(PIECES)] for d in range(2)]
-        x_scales = [[keep.tile([P, PIECE], U8, name=f"x_scales{d}_{i}", align_bytes=64) for i in range(PIECES)] for d in range(2)]
+        grouped = [keep.tile([P, WIDTH, PACK], BF16, name=f"grouped{d}", align_bytes=64) for d in range(2)]
+        codes = [keep.tile([P, WIDTH], U32, name=f"codes{d}", align_bytes=64) for d in range(2)]
+        scales = [keep.tile([P, WIDTH], U8, name=f"scales{d}", align_bytes=64) for d in range(2)]
+        picked = slice(P, P + V)
+        w_cols = [slice(0, P), slice(P + V, WIDTH)]
         pieces = [slice(i * PIECE, (i + 1) * PIECE) for i in range(PIECES)]
 
-        def interleave_w(d, m):
-            nc.scalar.copy(
-                out=w_grouped[d][m][:],
-                in_=w_raw[d][:, :, m * P : (m + 1) * P].rearrange("p j n -> p n j"),
-            )
+        def raw_walk(d, m):
+            return w_raw[d][:, :, m * P : (m + 1) * P].rearrange("p j (c i) -> p c j i", i=RUN)
 
-        def quantise_w(d, m):
+        def grouped_walk(d, m):
+            return grouped[d][:, w_cols[m], :].rearrange("p (c i) j -> p c j i", i=RUN)
+
+        def interleave_w(copy, d, m):
+            copy(out=grouped_walk(d, m), in_=raw_walk(d, m))
+
+        def quantise(d, cols):
             nc.vector.quantize_mx(
-                out=w_codes[d][m][:].bitcast(FP8X4),
-                scales=w_scales[d][m][:],
-                in_=w_grouped[d][m][:].rearrange("p n j -> p (n j)"),
+                out=codes[d][:, cols].bitcast(FP8X4),
+                scales=scales[d][:, cols],
+                in_=grouped[d][:, cols, :].rearrange("p c j -> p (c j)"),
             )
 
-        def gather(j, d):
-            nc.vector.tensor_copy(x_grouped[d][:, :, j], planes[j][:].indirect(halves[d]))
-
-        def quantise_x(d, i):
-            nc.vector.quantize_mx(
-                out=x_codes[d][i][:].bitcast(FP8X4),
-                scales=x_scales[d][i][:],
-                in_=x_grouped[d][:, pieces[i], :].rearrange("p v j -> p (v j)"),
-            )
+        def gather(j):
+            nc.vector.tensor_copy(grouped[0][:, picked, j], planes[j][:].indirect(halves[0]))
 
         def product(d, i, m):
             bank = psum.tile([P, PIECE], F32, name=f"bank{d}_{i}_{m}")
-            nc.tensor.matmul_mx(
-                out=bank[:],
-                lhsT=w_codes[d][m][:].bitcast(FP8X4),
-                lhsT_scale=w_scales[d][m][:],
-                rhs=x_codes[d][i][:].bitcast(FP8X4),
-                rhs_scale=x_scales[d][i][:],
-                start=True,
-                stop=True,
-            )
+            first = P + i * PIECE
+            cuts = [first, first + PIECE]
+            if m == 0 and first < FRONT < first + PIECE:
+                cuts.insert(1, FRONT)
+            for a, b in zip(cuts, cuts[1:]):
+                nc.tensor.matmul_mx(
+                    out=bank[:, a - first : b - first],
+                    lhsT=codes[d][:, w_cols[m]].bitcast(FP8X4),
+                    lhsT_scale=scales[d][:, w_cols[m]],
+                    rhs=codes[d][:, a:b].bitcast(FP8X4),
+                    rhs_scale=scales[d][:, a:b],
+                    start=True,
+                    stop=True,
+                )
             return bank
 
-        for m in range(M_TILES):
-            interleave_w(0, m)
-        for m in range(M_TILES):
-            quantise_w(0, m)
         for j in range(2):
             nc.vector.tensor_copy(staged_pair[:, j, :], planes[j][:].indirect(halves[1]))
-            gather(j, 0)
-        nc.scalar.copy(out=x_grouped[1][:, :, 0:2], in_=staged_pair[:].rearrange("p e v -> p v e"))
+            gather(j)
+        nc.scalar.copy(out=grouped[1][:, picked, 0:2], in_=staged_pair[:].rearrange("p e v -> p v e"))
         nc.vector.tensor_copy(staged[:], planes[last - 1][:].indirect(halves[1]))
-        nc.scalar.copy(out=x_grouped[1][:, :, last - 1], in_=staged[:])
-        gather(last - 1, 0)
+        nc.scalar.copy(out=grouped[1][:, picked, last - 1], in_=staged[:])
+        gather(last - 1)
         for c, chunk in enumerate(chunks):
             cast = nc.scalar.copy if c % 2 else nc.vector.tensor_copy
             cast(out=last_bf16[:, chunk], in_=planes[last][:, chunk])
-        gather(last, 0)
-        nc.scalar.activation(x_grouped[1][:, :, last], last_bf16[:].indirect(halves[1]), COPY)
-        for m in range(M_TILES):
-            interleave_w(1, m)
+        gather(last)
+        nc.scalar.activation(grouped[1][:, picked, last], last_bf16[:].indirect(halves[1]), COPY)
 
-        banks0 = {}
-        for i in range(PIECES):
-            quantise_x(0, i)
-            for m in range(M_TILES):
-                banks0[i, m] = product(0, i, m)
-        for i in range(PIECES):
-            quantise_x(1, i)
         for m in range(M_TILES):
-            quantise_w(1, m)
+            interleave_w(nc.vector.tensor_copy, 0, m)
+            interleave_w(nc.scalar.copy, 1, m)
+        for d in range(2):
+            quantise(d, slice(0, FRONT))
+            quantise(d, slice(FRONT, WIDTH))
+
+        tiles = [(i, m) for m in range(M_TILES) for i in range(PIECES)]
         y0 = {}
-        for m in range(M_TILES):
-            for i in range(PIECES):
-                y0[i, m] = keep.tile([P, PIECE], F32, name=f"y0_{i}_{m}")
-                nc.scalar.copy(out=y0[i, m][:], in_=banks0[i, m][:])
-        for m in range(M_TILES):
-            for i in range(PIECES):
-                bank = product(1, i, m)
-                result = keep.tile([P, PIECE], F32, name=f"result{i}_{m}")
-                nc.vector.tensor_tensor(result[:], bank[:], y0[i, m][:], MULT)
-                nc.sync.dma_start(out=out[m * P : (m + 1) * P, pieces[i]], in_=result[:])
+        for i, m in tiles:
+            bank = product(0, i, m)
+            y0[i, m] = keep.tile([P, PIECE], F32, name=f"y0_{i}_{m}")
+            nc.scalar.copy(out=y0[i, m][:], in_=bank[:])
+        for i, m in tiles:
+            bank = product(1, i, m)
+            result = keep.tile([P, PIECE], F32, name=f"result{i}_{m}")
+            nc.vector.tensor_tensor(result[:], bank[:], y0[i, m][:], MULT)
+            nc.sync.dma_start(out=out[m * P : (m + 1) * P, pieces[i]], in_=result[:])

@@ -9,7 +9,8 @@ PIECE = 256
 PIECES = V // PIECE
 WIDTH = V + N
 FRONT = 512
-LAST_CHUNKS = (2048, 1024, 512, 512)
+LAST_CHUNKS = (1024, 1024, 1024, 512, 512)
+ORDER = (2, 0, 1)
 
 FLOPS = 2 * K * N * S
 
@@ -30,7 +31,6 @@ def tile_picked_pair_lin_mul_sub_e_kernel(tc, xT, w, offs, out):
         tc.psum_pool(name="psum", bufs=1) as psum,
     ):
         offsets = keep.tile([P, S // 16], U16, name="offsets")
-        nc.sync.dma_start(offsets[:], offs)
         halves = [offsets[:, d * (V // 16) : (d + 1) * (V // 16)] for d in range(2)]
 
         w_raw = [keep.tile([P, PACK, N], F32, name=f"w_raw{d}") for d in range(2)]
@@ -40,14 +40,15 @@ def tile_picked_pair_lin_mul_sub_e_kernel(tc, xT, w, offs, out):
         starts = [sum(LAST_CHUNKS[:c]) for c in range(len(LAST_CHUNKS))]
         chunks = [slice(a, a + n) for a, n in zip(starts, LAST_CHUNKS)]
         x_rows = xT.rearrange("(p j) t -> p j t", j=PACK)
-        for j in range(last):
+        nc.sync.dma_start(out=planes[ORDER[0]][:], in_=x_rows[:, ORDER[0], :])
+        nc.sync.dma_start(offsets[:], offs)
+        for j in ORDER[1:]:
             nc.sync.dma_start(out=planes[j][:], in_=x_rows[:, j, :])
         for chunk in chunks:
             nc.sync.dma_start(out=planes[last][:, chunk], in_=x_rows[:, last, chunk])
         for d in range(2):
             nc.sync.dma_start(out=w_raw[d][:], in_=w[d].rearrange("(p j) n -> p j n", j=PACK))
 
-        staged_pair = keep.tile([P, 2, V], F32, name="staged_pair")
         staged = keep.tile([P, V], F32, name="staged")
         grouped = [keep.tile([P, WIDTH, PACK], BF16, name=f"grouped{d}", align_bytes=64) for d in range(2)]
         codes = [keep.tile([P, WIDTH], U32, name=f"codes{d}", align_bytes=64) for d in range(2)]
@@ -72,8 +73,8 @@ def tile_picked_pair_lin_mul_sub_e_kernel(tc, xT, w, offs, out):
                 in_=grouped[d][:, cols, :].rearrange("p c j -> p (c j)"),
             )
 
-        def gather(j):
-            nc.vector.tensor_copy(grouped[0][:, picked, j], planes[j][:].indirect(halves[0]))
+        def gather(j, d):
+            nc.vector.tensor_copy(grouped[d][:, picked, j], planes[j][:].indirect(halves[d]))
 
         def product(d, i, m):
             bank = psum.tile([P, PIECE], F32, name=f"bank{d}_{i}_{m}")
@@ -93,17 +94,16 @@ def tile_picked_pair_lin_mul_sub_e_kernel(tc, xT, w, offs, out):
                 )
             return bank
 
-        for j in range(2):
-            nc.vector.tensor_copy(staged_pair[:, j, :], planes[j][:].indirect(halves[1]))
-            gather(j)
-        nc.scalar.copy(out=grouped[1][:, picked, 0:2], in_=staged_pair[:].rearrange("p e v -> p v e"))
-        nc.vector.tensor_copy(staged[:], planes[last - 1][:].indirect(halves[1]))
-        nc.scalar.copy(out=grouped[1][:, picked, last - 1], in_=staged[:])
-        gather(last - 1)
+        nc.vector.tensor_copy(staged[:], planes[ORDER[0]][:].indirect(halves[1]))
+        nc.scalar.copy(out=grouped[1][:, picked, ORDER[0]], in_=staged[:])
+        gather(ORDER[0], 0)
+        for j in ORDER[1:]:
+            for d in range(2):
+                gather(j, d)
         for c, chunk in enumerate(chunks):
-            cast = nc.scalar.copy if c % 2 else nc.vector.tensor_copy
+            cast = nc.vector.tensor_copy if c == len(chunks) - 2 else nc.scalar.copy
             cast(out=last_bf16[:, chunk], in_=planes[last][:, chunk])
-        gather(last)
+        gather(last, 0)
         nc.scalar.activation(grouped[1][:, picked, last], last_bf16[:].indirect(halves[1]), COPY)
 
         for m in range(M_TILES):

@@ -10,6 +10,7 @@ PIECES = V // PIECE
 WIDTH = V + N
 FRONT = 512
 LAST_CHUNKS = (1024, 1024, 1024, 512, 512)
+LEAD = 64
 ORDER = (2, 0, 1)
 
 FLOPS = 2 * K * N * S
@@ -77,7 +78,7 @@ def tile_picked_pair_lin_mul_sub_e_kernel(tc, xT, w, offs, out):
             nc.vector.tensor_copy(grouped[d][:, picked, j], planes[j][:].indirect(halves[d]))
 
         def product(d, i, m):
-            bank = psum.tile([P, PIECE], F32, name=f"bank{d}_{i}_{m}")
+            bank = psum.tile([P, PIECE], F32, name=f"bank{d}_{i}_{m}", tag=f"bank{i}_{m}")
             first = P + i * PIECE
             cuts = [first, first + PIECE]
             if m == 0 and first < FRONT < first + PIECE:
@@ -100,9 +101,16 @@ def tile_picked_pair_lin_mul_sub_e_kernel(tc, xT, w, offs, out):
         for j in ORDER[1:]:
             for d in range(2):
                 gather(j, d)
-        for c, chunk in enumerate(chunks):
-            cast = nc.vector.tensor_copy if c == len(chunks) - 2 else nc.scalar.copy
-            cast(out=last_bf16[:, chunk], in_=planes[last][:, chunk])
+        wide = slice(0, starts[3])
+        for chunk in chunks[:3]:
+            rest = slice(chunk.start + LEAD, chunk.stop)
+            nc.scalar.copy(out=last_bf16[:, rest], in_=planes[last][:, rest])
+        nc.vector.tensor_copy(
+            out=last_bf16[:, wide].rearrange("p (c t) -> p c t", c=3)[:, :, 0:LEAD],
+            in_=planes[last][:, wide].rearrange("p (c t) -> p c t", c=3)[:, :, 0:LEAD],
+        )
+        nc.vector.tensor_copy(out=last_bf16[:, chunks[3]], in_=planes[last][:, chunks[3]])
+        nc.scalar.copy(out=last_bf16[:, chunks[4]], in_=planes[last][:, chunks[4]])
         gather(last, 0)
         nc.scalar.activation(grouped[1][:, picked, last], last_bf16[:].indirect(halves[1]), COPY)
 

@@ -5,12 +5,12 @@ P = 128
 PACK = 4
 RUN = 4
 M_TILES = N // P
-PIECE = 256
-PIECES = V // PIECE
+PIECES = (((0, 128), (128, 384), (384, 512)), ((0, 256), (256, 512)))
 WIDTH = V + N
 FRONT = 512
-LAST_CHUNKS = (1024, 1024, 1024, 512, 512)
-LEAD = 64
+LAST_CHUNKS = (1280, 1280, 1024, 512)
+LEAD = 32
+THIRD_VECTOR = 768
 ORDER = (2, 0, 1)
 
 FLOPS = 2 * K * N * S
@@ -56,7 +56,6 @@ def tile_picked_pair_lin_mul_sub_e_kernel(tc, xT, w, offs, out):
         scales = [keep.tile([P, WIDTH], U8, name=f"scales{d}", align_bytes=64) for d in range(2)]
         picked = slice(P, P + V)
         w_cols = [slice(0, P), slice(P + V, WIDTH)]
-        pieces = [slice(i * PIECE, (i + 1) * PIECE) for i in range(PIECES)]
 
         def raw_walk(d, m):
             return w_raw[d][:, :, m * P : (m + 1) * P].rearrange("p j (c i) -> p c j i", i=RUN)
@@ -77,22 +76,17 @@ def tile_picked_pair_lin_mul_sub_e_kernel(tc, xT, w, offs, out):
         def gather(j, d):
             nc.vector.tensor_copy(grouped[d][:, picked, j], planes[j][:].indirect(halves[d]))
 
-        def product(d, i, m):
-            bank = psum.tile([P, PIECE], F32, name=f"bank{d}_{i}_{m}", tag=f"bank{i}_{m}")
-            first = P + i * PIECE
-            cuts = [first, first + PIECE]
-            if m == 0 and first < FRONT < first + PIECE:
-                cuts.insert(1, FRONT)
-            for a, b in zip(cuts, cuts[1:]):
-                nc.tensor.matmul_mx(
-                    out=bank[:, a - first : b - first],
-                    lhsT=codes[d][:, w_cols[m]].bitcast(FP8X4),
-                    lhsT_scale=scales[d][:, w_cols[m]],
-                    rhs=codes[d][:, a:b].bitcast(FP8X4),
-                    rhs_scale=scales[d][:, a:b],
-                    start=True,
-                    stop=True,
-                )
+        def product(d, m, a, b):
+            bank = psum.tile([P, b - a], F32, name=f"bank{d}_{m}_{a}", tag=f"bank{m}_{a}")
+            nc.tensor.matmul_mx(
+                out=bank[:],
+                lhsT=codes[d][:, w_cols[m]].bitcast(FP8X4),
+                lhsT_scale=scales[d][:, w_cols[m]],
+                rhs=codes[d][:, P + a : P + b].bitcast(FP8X4),
+                rhs_scale=scales[d][:, P + a : P + b],
+                start=True,
+                stop=True,
+            )
             return bank
 
         nc.vector.tensor_copy(staged[:], planes[ORDER[0]][:].indirect(halves[1]))
@@ -101,16 +95,18 @@ def tile_picked_pair_lin_mul_sub_e_kernel(tc, xT, w, offs, out):
         for j in ORDER[1:]:
             for d in range(2):
                 gather(j, d)
-        wide = slice(0, starts[3])
-        for chunk in chunks[:3]:
+        wide = slice(0, starts[2])
+        for chunk in chunks[:2]:
             rest = slice(chunk.start + LEAD, chunk.stop)
             nc.scalar.copy(out=last_bf16[:, rest], in_=planes[last][:, rest])
         nc.vector.tensor_copy(
-            out=last_bf16[:, wide].rearrange("p (c t) -> p c t", c=3)[:, :, 0:LEAD],
-            in_=planes[last][:, wide].rearrange("p (c t) -> p c t", c=3)[:, :, 0:LEAD],
+            out=last_bf16[:, wide].rearrange("p (c t) -> p c t", c=2)[:, :, 0:LEAD],
+            in_=planes[last][:, wide].rearrange("p (c t) -> p c t", c=2)[:, :, 0:LEAD],
         )
-        nc.vector.tensor_copy(out=last_bf16[:, chunks[3]], in_=planes[last][:, chunks[3]])
-        nc.scalar.copy(out=last_bf16[:, chunks[4]], in_=planes[last][:, chunks[4]])
+        cut = starts[2] + THIRD_VECTOR
+        nc.vector.tensor_copy(out=last_bf16[:, starts[2] : cut], in_=planes[last][:, starts[2] : cut])
+        nc.scalar.copy(out=last_bf16[:, cut : starts[3]], in_=planes[last][:, cut : starts[3]])
+        nc.scalar.copy(out=last_bf16[:, chunks[3]], in_=planes[last][:, chunks[3]])
         gather(last, 0)
         nc.scalar.activation(grouped[1][:, picked, last], last_bf16[:].indirect(halves[1]), COPY)
 
@@ -121,14 +117,14 @@ def tile_picked_pair_lin_mul_sub_e_kernel(tc, xT, w, offs, out):
             quantise(d, slice(0, FRONT))
             quantise(d, slice(FRONT, WIDTH))
 
-        tiles = [(i, m) for m in range(M_TILES) for i in range(PIECES)]
+        tiles = [(m, a, b) for m in range(M_TILES) for a, b in PIECES[m]]
         y0 = {}
-        for i, m in tiles:
-            bank = product(0, i, m)
-            y0[i, m] = keep.tile([P, PIECE], F32, name=f"y0_{i}_{m}")
-            nc.scalar.copy(out=y0[i, m][:], in_=bank[:])
-        for i, m in tiles:
-            bank = product(1, i, m)
-            result = keep.tile([P, PIECE], F32, name=f"result{i}_{m}")
-            nc.vector.tensor_tensor(result[:], bank[:], y0[i, m][:], MULT)
-            nc.sync.dma_start(out=out[m * P : (m + 1) * P, pieces[i]], in_=result[:])
+        for m, a, b in tiles:
+            bank = product(0, m, a, b)
+            y0[m, a] = keep.tile([P, b - a], F32, name=f"y0_{m}_{a}")
+            nc.scalar.copy(out=y0[m, a][:], in_=bank[:])
+        for m, a, b in tiles:
+            bank = product(1, m, a, b)
+            result = keep.tile([P, b - a], F32, name=f"result{m}_{a}")
+            nc.vector.tensor_tensor(result[:], bank[:], y0[m, a][:], MULT)
+            nc.sync.dma_start(out=out[m * P : (m + 1) * P, a:b], in_=result[:])

@@ -4,14 +4,13 @@ K, T, S, V, N = 512, 4096, 1024, 512, 256
 P = 128
 PACK = 4
 RUN = 4
-M_TILES = N // P
-PIECES = (((0, 128), (128, 384), (384, 512)), ((0, 256), (256, 512)))
-WIDTH = V + N
-FRONT = 512
-LAST_CHUNKS = (1280, 1280, 1024, 512)
-LEAD = 32
-THIRD_VECTOR = 768
+QUARTER = S // 4
+GROUP = P + QUARTER
+WIDTH = 4 * GROUP
+CHUNKS = (1792, 1408, 640, 256)
+VECTOR_CASTS = (256, 1408, 384, 0)
 ORDER = (2, 0, 1)
+SHARE = 64
 
 FLOPS = 2 * K * N * S
 
@@ -22,6 +21,7 @@ U16 = mybir.dt.uint16
 U8 = mybir.dt.uint8
 FP8X4 = mybir.dt.float8_e4m3fn_x4
 MULT = mybir.AluOpType.mult
+ADD = mybir.AluOpType.add
 COPY = mybir.ActivationFunctionType.Copy
 
 
@@ -32,99 +32,112 @@ def tile_picked_pair_lin_mul_sub_e_kernel(tc, xT, w, offs, out):
         tc.psum_pool(name="psum", bufs=1) as psum,
     ):
         offsets = keep.tile([P, S // 16], U16, name="offsets")
-        halves = [offsets[:, d * (V // 16) : (d + 1) * (V // 16)] for d in range(2)]
+
+        def entries(a, b):
+            return offsets[:, a // 16 : b // 16]
 
         w_raw = [keep.tile([P, PACK, N], F32, name=f"w_raw{d}") for d in range(2)]
         planes = [keep.tile([P, T], F32, name=f"plane{j}") for j in range(PACK)]
         last = PACK - 1
         last_bf16 = keep.tile([P, T], BF16, name="last_bf16")
-        starts = [sum(LAST_CHUNKS[:c]) for c in range(len(LAST_CHUNKS))]
-        chunks = [slice(a, a + n) for a, n in zip(starts, LAST_CHUNKS)]
+        starts = [sum(CHUNKS[:c]) for c in range(len(CHUNKS))]
         x_rows = xT.rearrange("(p j) t -> p j t", j=PACK)
         nc.sync.dma_start(out=planes[ORDER[0]][:], in_=x_rows[:, ORDER[0], :])
         nc.sync.dma_start(offsets[:], offs)
         for j in ORDER[1:]:
             nc.sync.dma_start(out=planes[j][:], in_=x_rows[:, j, :])
-        for chunk in chunks:
-            nc.sync.dma_start(out=planes[last][:, chunk], in_=x_rows[:, last, chunk])
+        for a, n in zip(starts, CHUNKS):
+            nc.sync.dma_start(out=planes[last][:, a : a + n], in_=x_rows[:, last, a : a + n])
         for d in range(2):
             nc.sync.dma_start(out=w_raw[d][:], in_=w[d].rearrange("(p j) n -> p j n", j=PACK))
 
-        staged = keep.tile([P, V], F32, name="staged")
-        grouped = [keep.tile([P, WIDTH, PACK], BF16, name=f"grouped{d}", align_bytes=64) for d in range(2)]
-        codes = [keep.tile([P, WIDTH], U32, name=f"codes{d}", align_bytes=64) for d in range(2)]
-        scales = [keep.tile([P, WIDTH], U8, name=f"scales{d}", align_bytes=64) for d in range(2)]
-        picked = slice(P, P + V)
-        w_cols = [slice(0, P), slice(P + V, WIDTH)]
+        grouped = keep.tile([P, 4, GROUP, PACK], BF16, name="grouped", align_bytes=64)
+        codes = keep.tile([P, WIDTH], U32, name="codes", align_bytes=64)
+        scales = keep.tile([P, WIDTH], U8, name="scales", align_bytes=64)
 
-        def raw_walk(d, m):
-            return w_raw[d][:, :, m * P : (m + 1) * P].rearrange("p j (c i) -> p c j i", i=RUN)
+        def picked(q0, q1, j):
+            return grouped[:, q0:q1, P:GROUP, j]
 
-        def grouped_walk(d, m):
-            return grouped[d][:, w_cols[m], :].rearrange("p (c i) j -> p c j i", i=RUN)
+        def by_quarter(ap):
+            return ap.rearrange("p (q c) -> p q c", c=QUARTER)
 
-        def interleave_w(copy, d, m):
-            copy(out=grouped_walk(d, m), in_=raw_walk(d, m))
-
-        def quantise(d, cols):
-            nc.vector.quantize_mx(
-                out=codes[d][:, cols].bitcast(FP8X4),
-                scales=scales[d][:, cols],
-                in_=grouped[d][:, cols, :].rearrange("p c j -> p (c j)"),
+        def interleave_w(copy, d, m, a):
+            copy(
+                out=grouped[:, 2 * d + m, a:P, :].rearrange("p (c i) j -> p c j i", i=RUN),
+                in_=w_raw[d][:, :, m * P + a : (m + 1) * P].rearrange("p j (c i) -> p c j i", i=RUN),
             )
 
-        def gather(j, d):
-            nc.vector.tensor_copy(grouped[d][:, picked, j], planes[j][:].indirect(halves[d]))
+        def quantise(a, b):
+            nc.vector.quantize_mx(
+                out=codes[:, a:b].bitcast(FP8X4),
+                scales=scales[:, a:b],
+                in_=grouped[:].rearrange("p q c j -> p (q c j)")[:, PACK * a : PACK * b],
+            )
 
-        def product(d, m, a, b):
-            bank = psum.tile([P, b - a], F32, name=f"bank{d}_{m}_{a}", tag=f"bank{m}_{a}")
+        def product(d, m, a, b, tag):
+            bank = psum.tile([P, b - a], F32, name=f"bank{d}_{m}_{a}", tag=tag)
+            w_at = (2 * d + m) * GROUP
+            x_at = (2 * d + a // QUARTER) * GROUP + P + a % QUARTER
             nc.tensor.matmul_mx(
                 out=bank[:],
-                lhsT=codes[d][:, w_cols[m]].bitcast(FP8X4),
-                lhsT_scale=scales[d][:, w_cols[m]],
-                rhs=codes[d][:, P + a : P + b].bitcast(FP8X4),
-                rhs_scale=scales[d][:, P + a : P + b],
+                lhsT=codes[:, w_at : w_at + P].bitcast(FP8X4),
+                lhsT_scale=scales[:, w_at : w_at + P],
+                rhs=codes[:, x_at : x_at + b - a].bitcast(FP8X4),
+                rhs_scale=scales[:, x_at : x_at + b - a],
                 start=True,
                 stop=True,
             )
             return bank
 
-        nc.vector.tensor_copy(staged[:], planes[ORDER[0]][:].indirect(halves[1]))
-        nc.scalar.copy(out=grouped[1][:, picked, ORDER[0]], in_=staged[:])
-        gather(ORDER[0], 0)
-        for j in ORDER[1:]:
-            for d in range(2):
-                gather(j, d)
-        wide = slice(0, starts[2])
-        for chunk in chunks[:2]:
-            rest = slice(chunk.start + LEAD, chunk.stop)
-            nc.scalar.copy(out=last_bf16[:, rest], in_=planes[last][:, rest])
-        nc.vector.tensor_copy(
-            out=last_bf16[:, wide].rearrange("p (c t) -> p c t", c=2)[:, :, 0:LEAD],
-            in_=planes[last][:, wide].rearrange("p (c t) -> p c t", c=2)[:, :, 0:LEAD],
+        for j in ORDER:
+            dense = keep.tile([P, V], BF16, name=f"dense{j}")
+            nc.vector.tensor_copy(picked(0, 2, j), planes[j][:].indirect(entries(0, V)))
+            nc.scalar.activation(dense[:], planes[j][:].indirect(entries(V, S)), COPY)
+            lay = nc.scalar.copy if j == last - 1 else nc.vector.tensor_copy
+            lay(out=picked(2, 4, j), in_=by_quarter(dense[:]))
+
+        for a, n, share in zip(starts, CHUNKS, VECTOR_CASTS):
+            if share:
+                nc.vector.tensor_copy(out=last_bf16[:, a : a + share], in_=planes[last][:, a : a + share])
+            if share < n:
+                nc.scalar.copy(out=last_bf16[:, a + share : a + n], in_=planes[last][:, a + share : a + n])
+
+        nc.vector.tensor_copy(picked(0, 2, last), planes[last][:].indirect(entries(0, V)))
+        nc.scalar.activation(picked(2, 4, last), last_bf16[:].indirect(entries(V, S)), COPY)
+
+        nc.gpsimd.tensor_scalar(
+            grouped[:, 0:2, 0:SHARE, :],
+            w_raw[0][:].rearrange("p j (m c) -> p m c j", m=2)[:, :, 0:SHARE, :],
+            1.0,
+            0.0,
+            MULT,
+            ADD,
         )
-        cut = starts[2] + THIRD_VECTOR
-        nc.vector.tensor_copy(out=last_bf16[:, starts[2] : cut], in_=planes[last][:, starts[2] : cut])
-        nc.scalar.copy(out=last_bf16[:, cut : starts[3]], in_=planes[last][:, cut : starts[3]])
-        nc.scalar.copy(out=last_bf16[:, chunks[3]], in_=planes[last][:, chunks[3]])
-        gather(last, 0)
-        nc.scalar.activation(grouped[1][:, picked, last], last_bf16[:].indirect(halves[1]), COPY)
+        for m in range(2):
+            interleave_w(nc.vector.tensor_copy, 0, m, SHARE)
+            interleave_w(nc.scalar.copy, 1, m, 0)
+        for q in range(4):
+            quantise(q * GROUP, (q + 1) * GROUP)
 
-        for m in range(M_TILES):
-            interleave_w(nc.vector.tensor_copy, 0, m)
-            interleave_w(nc.scalar.copy, 1, m)
-        for d in range(2):
-            quantise(d, slice(0, FRONT))
-            quantise(d, slice(FRONT, WIDTH))
+        y0 = [keep.tile([P, V], F32, name=f"y0_{m}") for m in range(2)]
 
-        tiles = [(m, a, b) for m in range(M_TILES) for a, b in PIECES[m]]
-        y0 = {}
-        for m, a, b in tiles:
-            bank = product(0, m, a, b)
-            y0[m, a] = keep.tile([P, b - a], F32, name=f"y0_{m}_{a}")
-            nc.scalar.copy(out=y0[m, a][:], in_=bank[:])
-        for m, a, b in tiles:
-            bank = product(1, m, a, b)
+        def first_product(m, a, b):
+            bank = product(0, m, a, b, f"first{m}_{a}")
+            nc.scalar.copy(out=y0[m][:, a:b], in_=bank[:])
+
+        def second_product(m, a, b, tag):
+            bank = product(1, m, a, b, tag)
             result = keep.tile([P, b - a], F32, name=f"result{m}_{a}")
-            nc.vector.tensor_tensor(result[:], bank[:], y0[m, a][:], MULT)
+            nc.vector.tensor_tensor(result[:], bank[:], y0[m][:, a:b], MULT)
             nc.sync.dma_start(out=out[m * P : (m + 1) * P, a:b], in_=result[:])
+
+        first_product(0, 0, QUARTER)
+        first_product(1, 0, QUARTER)
+        first_product(0, QUARTER, V)
+        first_product(1, QUARTER, V)
+        second_product(0, 0, P, "first0_0")
+        second_product(0, P, QUARTER, "second0")
+        second_product(1, 0, QUARTER, "first1_0")
+        second_product(0, QUARTER, V, "second1")
+        second_product(1, QUARTER, QUARTER + P, "second2")
+        second_product(1, QUARTER + P, V, "second3")

@@ -4,13 +4,16 @@ K, T, S, V, N = 512, 4096, 1024, 512, 256
 P = 128
 PACK = 4
 RUN = 4
-QUARTER = S // 4
-GROUP = P + QUARTER
-WIDTH = 4 * GROUP
-CHUNKS = (1792, 1408, 640, 256)
-VECTOR_CASTS = (256, 1408, 384, 0)
-ORDER = (2, 0, 1)
-SHARE = 64
+LAST_CHUNKS = (1536, 1664, 640, 256)
+VECTOR_CASTS = (256, 1088, 416, 0)
+EARLY_SHARE = 48
+LATE_SHARE = 32
+W_AT = ((0, P + V), (2 * P + S, 3 * P + S))
+X_AT = (P, 2 * P + V)
+WIDTH = S + 4 * P
+CALL_ENDS = (512, 896, 1408, WIDTH)
+FIRST_PIECES = ((0, 0, 128), (0, 128, 384), (0, 384, 512), (1, 0, 256), (1, 256, 512))
+SECOND_PIECES = ((0, 0, 128), (0, 128, 256), (0, 256, 512), (1, 0, 256), (1, 256, 512))
 
 FLOPS = 2 * K * N * S
 
@@ -21,7 +24,6 @@ U16 = mybir.dt.uint16
 U8 = mybir.dt.uint8
 FP8X4 = mybir.dt.float8_e4m3fn_x4
 MULT = mybir.AluOpType.mult
-ADD = mybir.AluOpType.add
 COPY = mybir.ActivationFunctionType.Copy
 
 
@@ -32,112 +34,91 @@ def tile_picked_pair_lin_mul_sub_e_kernel(tc, xT, w, offs, out):
         tc.psum_pool(name="psum", bufs=1) as psum,
     ):
         offsets = keep.tile([P, S // 16], U16, name="offsets")
+        halves = [offsets[:, d * (V // 16) : (d + 1) * (V // 16)] for d in range(2)]
 
-        def entries(a, b):
-            return offsets[:, a // 16 : b // 16]
-
-        w_raw = [keep.tile([P, PACK, N], F32, name=f"w_raw{d}") for d in range(2)]
-        planes = [keep.tile([P, T], F32, name=f"plane{j}") for j in range(PACK)]
         last = PACK - 1
+        middle = keep.tile([P, 2, T], F32, name="middle")
+        first_plane = keep.tile([P, T], F32, name="first_plane")
+        last_plane = keep.tile([P, T], F32, name="last_plane")
         last_bf16 = keep.tile([P, T], BF16, name="last_bf16")
-        starts = [sum(CHUNKS[:c]) for c in range(len(CHUNKS))]
+        w_raw = [keep.tile([P, PACK, N], F32, name=f"w_raw{d}") for d in range(2)]
+        starts = [sum(LAST_CHUNKS[:c]) for c in range(len(LAST_CHUNKS))]
+        chunks = [slice(a, a + n) for a, n in zip(starts, LAST_CHUNKS)]
         x_rows = xT.rearrange("(p j) t -> p j t", j=PACK)
-        nc.sync.dma_start(out=planes[ORDER[0]][:], in_=x_rows[:, ORDER[0], :])
+        nc.sync.dma_start(out=middle[:], in_=x_rows[:, 1:last, :])
         nc.sync.dma_start(offsets[:], offs)
-        for j in ORDER[1:]:
-            nc.sync.dma_start(out=planes[j][:], in_=x_rows[:, j, :])
-        for a, n in zip(starts, CHUNKS):
-            nc.sync.dma_start(out=planes[last][:, a : a + n], in_=x_rows[:, last, a : a + n])
+        nc.sync.dma_start(out=first_plane[:], in_=x_rows[:, 0, :])
+        for chunk in chunks:
+            nc.sync.dma_start(out=last_plane[:, chunk], in_=x_rows[:, last, chunk])
         for d in range(2):
             nc.sync.dma_start(out=w_raw[d][:], in_=w[d].rearrange("(p j) n -> p j n", j=PACK))
 
-        grouped = keep.tile([P, 4, GROUP, PACK], BF16, name="grouped", align_bytes=64)
+        grouped = keep.tile([P, WIDTH, PACK], BF16, name="grouped", align_bytes=64)
         codes = keep.tile([P, WIDTH], U32, name="codes", align_bytes=64)
         scales = keep.tile([P, WIDTH], U8, name="scales", align_bytes=64)
+        picked = [slice(at, at + V) for at in X_AT]
 
-        def picked(q0, q1, j):
-            return grouped[:, q0:q1, P:GROUP, j]
-
-        def by_quarter(ap):
-            return ap.rearrange("p (q c) -> p q c", c=QUARTER)
-
-        def interleave_w(copy, d, m, a):
+        def interleave_w(copy, d, m, a, b):
+            at = W_AT[d][m]
             copy(
-                out=grouped[:, 2 * d + m, a:P, :].rearrange("p (c i) j -> p c j i", i=RUN),
-                in_=w_raw[d][:, :, m * P + a : (m + 1) * P].rearrange("p j (c i) -> p c j i", i=RUN),
+                out=grouped[:, at + a : at + b, :].rearrange("p (c i) j -> p c j i", i=RUN),
+                in_=w_raw[d][:, :, m * P + a : m * P + b].rearrange("p j (c i) -> p c j i", i=RUN),
             )
 
-        def quantise(a, b):
+        def quantise(call):
+            cols = slice(CALL_ENDS[call - 1] if call else 0, CALL_ENDS[call])
             nc.vector.quantize_mx(
-                out=codes[:, a:b].bitcast(FP8X4),
-                scales=scales[:, a:b],
-                in_=grouped[:].rearrange("p q c j -> p (q c j)")[:, PACK * a : PACK * b],
+                out=codes[:, cols].bitcast(FP8X4),
+                scales=scales[:, cols],
+                in_=grouped[:, cols, :].rearrange("p c j -> p (c j)"),
             )
 
-        def product(d, m, a, b, tag):
-            bank = psum.tile([P, b - a], F32, name=f"bank{d}_{m}_{a}", tag=tag)
-            w_at = (2 * d + m) * GROUP
-            x_at = (2 * d + a // QUARTER) * GROUP + P + a % QUARTER
+        def product(d, piece, m, a, b):
+            bank = psum.tile([P, b - a], F32, name=f"bank{d}_{piece}", tag=f"bank{piece}")
+            w_cols = slice(W_AT[d][m], W_AT[d][m] + P)
+            x_cols = slice(X_AT[d] + a, X_AT[d] + b)
             nc.tensor.matmul_mx(
                 out=bank[:],
-                lhsT=codes[:, w_at : w_at + P].bitcast(FP8X4),
-                lhsT_scale=scales[:, w_at : w_at + P],
-                rhs=codes[:, x_at : x_at + b - a].bitcast(FP8X4),
-                rhs_scale=scales[:, x_at : x_at + b - a],
+                lhsT=codes[:, w_cols].bitcast(FP8X4),
+                lhsT_scale=scales[:, w_cols],
+                rhs=codes[:, x_cols].bitcast(FP8X4),
+                rhs_scale=scales[:, x_cols],
                 start=True,
                 stop=True,
             )
             return bank
 
-        for j in ORDER:
-            dense = keep.tile([P, V], BF16, name=f"dense{j}")
-            nc.vector.tensor_copy(picked(0, 2, j), planes[j][:].indirect(entries(0, V)))
-            nc.scalar.activation(dense[:], planes[j][:].indirect(entries(V, S)), COPY)
-            lay = nc.scalar.copy if j == last - 1 else nc.vector.tensor_copy
-            lay(out=picked(2, 4, j), in_=by_quarter(dense[:]))
-
-        for a, n, share in zip(starts, CHUNKS, VECTOR_CASTS):
+        dense = keep.tile([P, last, V], F32, name="dense")
+        for j in (1, 2, 0):
+            window = middle[:, j - 1, :] if j else first_plane[:]
+            nc.vector.tensor_copy(grouped[:, picked[0], j], window.indirect(halves[0]))
+            nc.scalar.activation(dense[:, j, :], window.indirect(halves[1]), COPY)
+        nc.vector.tensor_copy(out=grouped[:, picked[1], 0:last], in_=dense[:].rearrange("p j c -> p c j"))
+        for chunk, share in zip(chunks, VECTOR_CASTS):
+            cut = chunk.start + share
             if share:
-                nc.vector.tensor_copy(out=last_bf16[:, a : a + share], in_=planes[last][:, a : a + share])
-            if share < n:
-                nc.scalar.copy(out=last_bf16[:, a + share : a + n], in_=planes[last][:, a + share : a + n])
+                nc.vector.tensor_copy(out=last_bf16[:, chunk.start : cut], in_=last_plane[:, chunk.start : cut])
+            nc.scalar.copy(out=last_bf16[:, cut : chunk.stop], in_=last_plane[:, cut : chunk.stop])
+        nc.vector.tensor_copy(grouped[:, picked[0], last], last_plane[:].indirect(halves[0]))
+        nc.scalar.activation(grouped[:, picked[1], last], last_bf16[:].indirect(halves[1]), COPY)
 
-        nc.vector.tensor_copy(picked(0, 2, last), planes[last][:].indirect(entries(0, V)))
-        nc.scalar.activation(picked(2, 4, last), last_bf16[:].indirect(entries(V, S)), COPY)
-
-        nc.gpsimd.tensor_scalar(
-            grouped[:, 0:2, 0:SHARE, :],
-            w_raw[0][:].rearrange("p j (m c) -> p m c j", m=2)[:, :, 0:SHARE, :],
-            1.0,
-            0.0,
-            MULT,
-            ADD,
-        )
-        for m in range(2):
-            interleave_w(nc.vector.tensor_copy, 0, m, SHARE)
-            interleave_w(nc.scalar.copy, 1, m, 0)
-        for q in range(4):
-            quantise(q * GROUP, (q + 1) * GROUP)
+        interleave_w(nc.vector.tensor_copy, 0, 0, 0, P)
+        interleave_w(nc.vector.tensor_copy, 0, 1, 0, P - EARLY_SHARE)
+        interleave_w(nc.scalar.copy, 0, 1, P - EARLY_SHARE, P)
+        interleave_w(nc.scalar.copy, 1, 0, 0, P)
+        interleave_w(nc.scalar.copy, 1, 1, 0, P - LATE_SHARE)
+        quantise(0)
+        quantise(1)
+        interleave_w(nc.vector.tensor_copy, 1, 1, P - LATE_SHARE, P)
+        quantise(2)
+        quantise(3)
 
         y0 = [keep.tile([P, V], F32, name=f"y0_{m}") for m in range(2)]
-
-        def first_product(m, a, b):
-            bank = product(0, m, a, b, f"first{m}_{a}")
+        for piece, (m, a, b) in enumerate(FIRST_PIECES):
+            bank = product(0, piece, m, a, b)
             nc.scalar.copy(out=y0[m][:, a:b], in_=bank[:])
-
-        def second_product(m, a, b, tag):
-            bank = product(1, m, a, b, tag)
-            result = keep.tile([P, b - a], F32, name=f"result{m}_{a}")
+        for piece, (m, a, b) in enumerate(SECOND_PIECES):
+            bank = product(1, piece, m, a, b)
+            result = keep.tile([P, b - a], F32, name=f"result{piece}")
             nc.vector.tensor_tensor(result[:], bank[:], y0[m][:, a:b], MULT)
             nc.sync.dma_start(out=out[m * P : (m + 1) * P, a:b], in_=result[:])
-
-        first_product(0, 0, QUARTER)
-        first_product(1, 0, QUARTER)
-        first_product(0, QUARTER, V)
-        first_product(1, QUARTER, V)
-        second_product(0, 0, P, "first0_0")
-        second_product(0, P, QUARTER, "second0")
-        second_product(1, 0, QUARTER, "first1_0")
-        second_product(0, QUARTER, V, "second1")
-        second_product(1, QUARTER, QUARTER + P, "second2")
-        second_product(1, QUARTER + P, V, "second3")

@@ -12,8 +12,8 @@ W_AT = ((0, P + V), (2 * P + S, 3 * P + S))
 X_AT = (P, 2 * P + V)
 WIDTH = S + 4 * P
 CALL_ENDS = (512, 896, 1408, WIDTH)
-FIRST_PIECES = ((0, 0, 128), (0, 128, 384), (0, 384, 512), (1, 0, 256), (1, 256, 512))
-SECOND_PIECES = ((0, 0, 128), (0, 128, 256), (0, 256, 512), (1, 0, 256), (1, 256, 512))
+PIECES = ((0, 0, 128), (0, 128, 256), (0, 256, 384), (0, 384, 512), (1, 0, 256), (1, 256, 512))
+STORES = ((0, 0, 128), (0, 128, 256), (0, 256, 512), (1, 0, 256), (1, 256, 512))
 
 FLOPS = 2 * K * N * S
 
@@ -114,11 +114,12 @@ def tile_picked_pair_lin_mul_sub_e_kernel(tc, xT, w, offs, out):
         quantise(3)
 
         y0 = [keep.tile([P, V], F32, name=f"y0_{m}") for m in range(2)]
-        for piece, (m, a, b) in enumerate(FIRST_PIECES):
-            bank = product(0, piece, m, a, b)
+        for place, (m, a, b) in enumerate(PIECES):
+            bank = product(0, place, m, a, b)
             nc.scalar.copy(out=y0[m][:, a:b], in_=bank[:])
-        for piece, (m, a, b) in enumerate(SECOND_PIECES):
-            bank = product(1, piece, m, a, b)
-            result = keep.tile([P, b - a], F32, name=f"result{piece}")
-            nc.vector.tensor_tensor(result[:], bank[:], y0[m][:, a:b], MULT)
-            nc.sync.dma_start(out=out[m * P : (m + 1) * P, a:b], in_=result[:])
+        result = [keep.tile([P, V], F32, name=f"result{m}") for m in range(2)]
+        for place, (m, a, b) in enumerate(PIECES):
+            bank = product(1, place, m, a, b)
+            nc.vector.tensor_tensor(result[m][:, a:b], bank[:], y0[m][:, a:b], MULT)
+        for m, a, b in STORES:
+            nc.sync.dma_start(out=out[m * P : (m + 1) * P, a:b], in_=result[m][:, a:b])

@@ -4,16 +4,6 @@ K, T, S, V, N = 512, 4096, 1024, 512, 256
 P = 128
 PACK = 4
 RUN = 4
-LAST_CHUNKS = (1536, 1664, 640, 256)
-VECTOR_CASTS = (256, 1088, 416, 0)
-EARLY_SHARE = 48
-LATE_SHARE = 32
-W_AT = ((0, P + V), (2 * P + S, 3 * P + S))
-X_AT = (P, 2 * P + V)
-WIDTH = S + 4 * P
-CALL_ENDS = (512, 896, 1408, WIDTH)
-PIECES = ((0, 0, 128), (0, 128, 256), (0, 256, 384), (0, 384, 512), (1, 0, 256), (1, 256, 512))
-STORES = ((0, 0, 128), (0, 128, 256), (0, 256, 512), (1, 0, 256), (1, 256, 512))
 
 FLOPS = 2 * K * N * S
 
@@ -34,92 +24,107 @@ def tile_picked_pair_lin_mul_sub_e_kernel(tc, xT, w, offs, out):
         tc.psum_pool(name="psum", bufs=1) as psum,
     ):
         offsets = keep.tile([P, S // 16], U16, name="offsets")
-        halves = [offsets[:, d * (V // 16) : (d + 1) * (V // 16)] for d in range(2)]
+
+        def entries(a, b):
+            return offsets[:, a // 16 : b // 16]
 
         last = PACK - 1
         middle = keep.tile([P, 2, T], F32, name="middle")
         first_plane = keep.tile([P, T], F32, name="first_plane")
         last_plane = keep.tile([P, T], F32, name="last_plane")
-        last_bf16 = keep.tile([P, T], BF16, name="last_bf16")
         w_raw = [keep.tile([P, PACK, N], F32, name=f"w_raw{d}") for d in range(2)]
-        starts = [sum(LAST_CHUNKS[:c]) for c in range(len(LAST_CHUNKS))]
-        chunks = [slice(a, a + n) for a, n in zip(starts, LAST_CHUNKS)]
         x_rows = xT.rearrange("(p j) t -> p j t", j=PACK)
         nc.sync.dma_start(out=middle[:], in_=x_rows[:, 1:last, :])
         nc.sync.dma_start(offsets[:], offs)
         nc.sync.dma_start(out=first_plane[:], in_=x_rows[:, 0, :])
-        for chunk in chunks:
-            nc.sync.dma_start(out=last_plane[:, chunk], in_=x_rows[:, last, chunk])
+        nc.sync.dma_start(out=last_plane[:], in_=x_rows[:, last, :])
         for d in range(2):
             nc.sync.dma_start(out=w_raw[d][:], in_=w[d].rearrange("(p j) n -> p j n", j=PACK))
 
-        grouped = keep.tile([P, WIDTH, PACK], BF16, name="grouped", align_bytes=64)
-        codes = keep.tile([P, WIDTH], U32, name="codes", align_bytes=64)
-        scales = keep.tile([P, WIDTH], U8, name="scales", align_bytes=64)
-        picked = [slice(at, at + V) for at in X_AT]
+        front, back = 384 // PACK, 128 // PACK
+        width = V + N
+        tile0 = keep.tile([P, (front + width + back) * PACK], BF16, name="tile0", align_bytes=64)
+        tile1 = keep.tile([P, width * PACK], BF16, name="tile1", align_bytes=64)
+        grouped = [
+            tile0[:, front * PACK : (front + width) * PACK].rearrange("p (c j) -> p c j", j=PACK),
+            tile1[:].rearrange("p (c j) -> p c j", j=PACK),
+        ]
+        codes = [keep.tile([P, width], U32, name=f"codes{d}", align_bytes=64) for d in range(2)]
+        scales = [keep.tile([P, width], U8, name=f"scales{d}", align_bytes=64) for d in range(2)]
+        w_at = ((0, P + V), (256, 640))
 
-        def interleave_w(copy, d, m, a, b):
-            at = W_AT[d][m]
-            copy(
-                out=grouped[:, at + a : at + b, :].rearrange("p (c i) j -> p c j i", i=RUN),
-                in_=w_raw[d][:, :, m * P + a : m * P + b].rearrange("p j (c i) -> p c j i", i=RUN),
+        def x_at(d, v):
+            if d == 0:
+                return P + v
+            return v if v < 256 else v + P
+
+        def interleave_w(d, m):
+            at = w_at[d][m]
+            nc.scalar.copy(
+                out=grouped[d][:, at : at + P, :].rearrange("p (c i) j -> p c j i", i=RUN),
+                in_=w_raw[d][:, :, m * P : (m + 1) * P].rearrange("p j (c i) -> p c j i", i=RUN),
             )
 
-        def quantise(call):
-            cols = slice(CALL_ENDS[call - 1] if call else 0, CALL_ENDS[call])
+        def quantise(d, a, b):
             nc.vector.quantize_mx(
-                out=codes[:, cols].bitcast(FP8X4),
-                scales=scales[:, cols],
-                in_=grouped[:, cols, :].rearrange("p c j -> p (c j)"),
+                out=codes[d][:, a:b].bitcast(FP8X4),
+                scales=scales[d][:, a:b],
+                in_=grouped[d][:, a:b, :].rearrange("p c j -> p (c j)"),
             )
 
-        def product(d, piece, m, a, b):
-            bank = psum.tile([P, b - a], F32, name=f"bank{d}_{piece}", tag=f"bank{piece}")
-            w_cols = slice(W_AT[d][m], W_AT[d][m] + P)
-            x_cols = slice(X_AT[d] + a, X_AT[d] + b)
+        def product(bank, d, m, a, b):
+            w_cols = slice(w_at[d][m], w_at[d][m] + P)
+            x_cols = slice(x_at(d, a), x_at(d, a) + b - a)
             nc.tensor.matmul_mx(
-                out=bank[:],
-                lhsT=codes[:, w_cols].bitcast(FP8X4),
-                lhsT_scale=scales[:, w_cols],
-                rhs=codes[:, x_cols].bitcast(FP8X4),
-                rhs_scale=scales[:, x_cols],
+                out=bank,
+                lhsT=codes[d][:, w_cols].bitcast(FP8X4),
+                lhsT_scale=scales[d][:, w_cols],
+                rhs=codes[d][:, x_cols].bitcast(FP8X4),
+                rhs_scale=scales[d][:, x_cols],
                 start=True,
                 stop=True,
             )
-            return bank
 
+        x0 = grouped[0][:, P : P + V, :]
+        x1 = grouped[1].rearrange("p (h c) j -> p h c j", h=2)[:, :, 0:256, :]
         dense = keep.tile([P, last, V], F32, name="dense")
         for j in (1, 2, 0):
             window = middle[:, j - 1, :] if j else first_plane[:]
-            nc.vector.tensor_copy(grouped[:, picked[0], j], window.indirect(halves[0]))
-            nc.scalar.activation(dense[:, j, :], window.indirect(halves[1]), COPY)
-        nc.vector.tensor_copy(out=grouped[:, picked[1], 0:last], in_=dense[:].rearrange("p j c -> p c j"))
-        for chunk, share in zip(chunks, VECTOR_CASTS):
-            cut = chunk.start + share
-            if share:
-                nc.vector.tensor_copy(out=last_bf16[:, chunk.start : cut], in_=last_plane[:, chunk.start : cut])
-            nc.scalar.copy(out=last_bf16[:, cut : chunk.stop], in_=last_plane[:, cut : chunk.stop])
-        nc.vector.tensor_copy(grouped[:, picked[0], last], last_plane[:].indirect(halves[0]))
-        nc.scalar.activation(grouped[:, picked[1], last], last_bf16[:].indirect(halves[1]), COPY)
+            nc.vector.tensor_copy(x0[:, :, j], window.indirect(entries(0, V)))
+            nc.scalar.activation(dense[:, j, :], window.indirect(entries(V, S)), COPY)
+        nc.vector.tensor_copy(out=x1[:, :, :, 0:last], in_=dense[:].rearrange("p j (h c) -> p h c j", h=2))
 
-        interleave_w(nc.vector.tensor_copy, 0, 0, 0, P)
-        interleave_w(nc.vector.tensor_copy, 0, 1, 0, P - EARLY_SHARE)
-        interleave_w(nc.scalar.copy, 0, 1, P - EARLY_SHARE, P)
-        interleave_w(nc.scalar.copy, 1, 0, 0, P)
-        interleave_w(nc.scalar.copy, 1, 1, 0, P - LATE_SHARE)
-        quantise(0)
-        quantise(1)
-        interleave_w(nc.vector.tensor_copy, 1, 1, P - LATE_SHARE, P)
-        quantise(2)
-        quantise(3)
+        nc.vector.tensor_copy(x0[:, :, last], last_plane[:].indirect(entries(0, V)))
+        behind = (front + width) * PACK
+        nc.scalar.activation(tile0[:, 0:384], last_plane[:].indirect(entries(V, V + 384)), COPY)
+        nc.scalar.activation(tile0[:, behind : behind + 128], last_plane[:].indirect(entries(V + 384, S)), COPY)
+        nc.vector.tensor_copy(out=x1[:, 0, :, last], in_=tile0[:, 0:256])
+        interleave_w(0, 0)
+        interleave_w(0, 1)
+        quantise(0, 0, 512)
+        quantise(0, 512, width)
+        both = tile0[:, 256 : behind + 128].rearrange("p (g c) -> p g c", c=P)
+        nc.vector.tensor_copy(
+            out=x1[:, 1, :, last].rearrange("p (g c) -> p g c", c=P),
+            in_=both[:, 0 :: (behind - 256) // P, :],
+        )
+        interleave_w(1, 0)
+        interleave_w(1, 1)
+        quantise(1, 0, 384)
+        quantise(1, 384, 640)
+        quantise(1, 640, width)
 
         y0 = [keep.tile([P, V], F32, name=f"y0_{m}") for m in range(2)]
-        for place, (m, a, b) in enumerate(PIECES):
-            bank = product(0, place, m, a, b)
-            nc.scalar.copy(out=y0[m][:, a:b], in_=bank[:])
+        for place, (m, cuts) in enumerate(((0, (0, 256)), (0, (256, 384, 512)), (1, (0, 256)), (1, (256, 512)))):
+            bank = psum.tile([P, 256], F32, name=f"y0_bank{place}", tag=f"bank{place}")
+            for a, b in zip(cuts, cuts[1:]):
+                product(bank[:, a - cuts[0] : b - cuts[0]], 0, m, a, b)
+            nc.scalar.copy(out=y0[m][:, cuts[0] : cuts[-1]], in_=bank[:])
         result = [keep.tile([P, V], F32, name=f"result{m}") for m in range(2)]
-        for place, (m, a, b) in enumerate(PIECES):
-            bank = product(1, place, m, a, b)
-            nc.vector.tensor_tensor(result[m][:, a:b], bank[:], y0[m][:, a:b], MULT)
-        for m, a, b in STORES:
+        pieces = ((0, 0, 128, 0), (0, 128, 256, 4), (0, 256, 384, 1), (0, 384, 512, 5), (1, 0, 256, 2), (1, 256, 512, 3))
+        for m, a, b, place in pieces:
+            bank = psum.tile([P, 256], F32, name=f"y1_bank{place}", tag=f"bank{place}")
+            product(bank[:, 0 : b - a], 1, m, a, b)
+            nc.vector.tensor_tensor(result[m][:, a:b], bank[:, 0 : b - a], y0[m][:, a:b], MULT)
+        for m, a, b in ((0, 0, 128), (0, 128, 256), (0, 256, 512), (1, 0, 256), (1, 256, 512)):
             nc.sync.dma_start(out=out[m * P : (m + 1) * P, a:b], in_=result[m][:, a:b])

@@ -29,10 +29,11 @@ def tile_picked_pair_lin_mul_sub_e_kernel(tc, xT, w, offs, out):
             return offsets[:, a // 16 : b // 16]
 
         last = PACK - 1
+        half = V // 2
         middle = keep.tile([P, 2, T], F32, name="middle")
         first_plane = keep.tile([P, T], F32, name="first_plane")
         last_plane = keep.tile([P, T], F32, name="last_plane")
-        w_raw = [keep.tile([P, PACK, N], F32, name=f"w_raw{d}") for d in range(2)]
+        w_raw = [keep.tile([P, PACK, N], F32, name=f"w_raw{d}", tag=f"shared{d}", align_bytes=64) for d in range(2)]
         x_rows = xT.rearrange("(p j) t -> p j t", j=PACK)
         nc.sync.dma_start(out=middle[:], in_=x_rows[:, 1:last, :])
         nc.sync.dma_start(offsets[:], offs)
@@ -41,78 +42,73 @@ def tile_picked_pair_lin_mul_sub_e_kernel(tc, xT, w, offs, out):
         for d in range(2):
             nc.sync.dma_start(out=w_raw[d][:], in_=w[d].rearrange("(p j) n -> p j n", j=PACK))
 
-        front, back = 384 // PACK, 128 // PACK
-        width = V + N
-        tile0 = keep.tile([P, (front + width + back) * PACK], BF16, name="tile0", align_bytes=64)
-        tile1 = keep.tile([P, width * PACK], BF16, name="tile1", align_bytes=64)
-        grouped = [
-            tile0[:, front * PACK : (front + width) * PACK].rearrange("p (c j) -> p c j", j=PACK),
-            tile1[:].rearrange("p (c j) -> p c j", j=PACK),
-        ]
-        codes = [keep.tile([P, width], U32, name=f"codes{d}", align_bytes=64) for d in range(2)]
-        scales = [keep.tile([P, width], U8, name=f"scales{d}", align_bytes=64) for d in range(2)]
-        w_at = ((0, P + V), (256, 640))
-
-        def x_at(d, v):
-            if d == 0:
-                return P + v
-            return v if v < 256 else v + P
+        tile0 = keep.tile([P, V + N, PACK], BF16, name="tile0", align_bytes=64)
+        tile1 = keep.tile([P, V + N + P, PACK], BF16, name="tile1", align_bytes=64)
+        flat1 = tile1[:].rearrange("p c j -> p (c j)")
+        w_in = ((tile0[:, 0:P, :], tile0[:, P + V :, :]), (tile1[:, 352:480, :], tile1[:, 768:, :]))
+        x0 = tile0[:, P : P + V, :]
+        x1 = [tile1[:, 96:352, :], tile1[:, 512:768, :]]
 
         def interleave_w(d, m):
-            at = w_at[d][m]
             nc.scalar.copy(
-                out=grouped[d][:, at : at + P, :].rearrange("p (c i) j -> p c j i", i=RUN),
+                out=w_in[d][m].rearrange("p (c i) j -> p c j i", i=RUN),
                 in_=w_raw[d][:, :, m * P : (m + 1) * P].rearrange("p j (c i) -> p c j i", i=RUN),
             )
 
-        def quantise(d, a, b):
-            nc.vector.quantize_mx(
-                out=codes[d][:, a:b].bitcast(FP8X4),
-                scales=scales[d][:, a:b],
-                in_=grouped[d][:, a:b, :].rearrange("p c j -> p (c j)"),
-            )
+        def quantise(codes, scales, values):
+            nc.vector.quantize_mx(out=codes.bitcast(FP8X4), scales=scales, in_=values.rearrange("p c j -> p (c j)"))
 
-        def product(bank, d, m, a, b):
-            w_cols = slice(w_at[d][m], w_at[d][m] + P)
-            x_cols = slice(x_at(d, a), x_at(d, a) + b - a)
-            nc.tensor.matmul_mx(
-                out=bank,
-                lhsT=codes[d][:, w_cols].bitcast(FP8X4),
-                lhsT_scale=scales[d][:, w_cols],
-                rhs=codes[d][:, x_cols].bitcast(FP8X4),
-                rhs_scale=scales[d][:, x_cols],
-                start=True,
-                stop=True,
-            )
-
-        x0 = grouped[0][:, P : P + V, :]
-        x1 = grouped[1].rearrange("p (h c) j -> p h c j", h=2)[:, :, 0:256, :]
         dense = keep.tile([P, last, V], F32, name="dense")
         for j in (1, 2, 0):
             window = middle[:, j - 1, :] if j else first_plane[:]
             nc.vector.tensor_copy(x0[:, :, j], window.indirect(entries(0, V)))
             nc.scalar.activation(dense[:, j, :], window.indirect(entries(V, S)), COPY)
-        nc.vector.tensor_copy(out=x1[:, :, :, 0:last], in_=dense[:].rearrange("p j (h c) -> p h c j", h=2))
+        for h in range(2):
+            nc.vector.tensor_copy(
+                out=x1[h][:, :, 0:last], in_=dense[:, :, h * half : (h + 1) * half].rearrange("p j c -> p c j")
+            )
 
         nc.vector.tensor_copy(x0[:, :, last], last_plane[:].indirect(entries(0, V)))
-        behind = (front + width) * PACK
-        nc.scalar.activation(tile0[:, 0:384], last_plane[:].indirect(entries(V, V + 384)), COPY)
-        nc.scalar.activation(tile0[:, behind : behind + 128], last_plane[:].indirect(entries(V + 384, S)), COPY)
-        nc.vector.tensor_copy(out=x1[:, 0, :, last], in_=tile0[:, 0:256])
+        nc.scalar.activation(flat1[:, 0:384], last_plane[:].indirect(entries(V, V + 384)), COPY)
+        nc.scalar.activation(flat1[:, 1920:2048], last_plane[:].indirect(entries(V + 384, S)), COPY)
+        nc.vector.tensor_copy(out=x1[0][:, :, last], in_=flat1[:, 0:half])
         interleave_w(0, 0)
         interleave_w(0, 1)
-        quantise(0, 0, 512)
-        quantise(0, 512, width)
-        both = tile0[:, 256 : behind + 128].rearrange("p (g c) -> p g c", c=P)
-        nc.vector.tensor_copy(
-            out=x1[:, 1, :, last].rearrange("p (g c) -> p g c", c=P),
-            in_=both[:, 0 :: (behind - 256) // P, :],
-        )
+        codes0 = keep.tile([P, V + N], U32, name="codes0", align_bytes=64)
+        scales0 = keep.tile([P, V + N], U8, name="scales0", align_bytes=64)
+        quantise(codes0[:, 0:512], scales0[:, 0:512], tile0[:, 0:512, :])
+        quantise(codes0[:, 512:], scales0[:, 512:], tile0[:, 512:, :])
+        scales1 = keep.tile([P, V + N], U8, name="scales1", align_bytes=64)
+        w1_codes = keep.tile([P, N], U32, name="w1_codes", align_bytes=64)
+        x1a_codes = keep.tile([P, half], U32, name="x1a_codes", tag="shared0", align_bytes=64)
+        quantise(x1a_codes[:], scales1[:, 0:half], x1[0])
         interleave_w(1, 0)
+        quantise(w1_codes[:, 0:P], scales1[:, V : V + P], w_in[1][0])
+        staged = flat1[:, half:2048].rearrange("p (g c) -> p g c", c=P)
+        nc.vector.tensor_copy(out=x1[1][:, :, last].rearrange("p (g c) -> p g c", c=P), in_=staged[:, 0::13, :])
         interleave_w(1, 1)
-        quantise(1, 0, 384)
-        quantise(1, 384, 640)
-        quantise(1, 640, width)
+        quantise(w1_codes[:, P:], scales1[:, V + P :], w_in[1][1])
+        x1b_codes = keep.tile([P, half], U32, name="x1b_codes", tag="shared1", align_bytes=64)
+        quantise(x1b_codes[:], scales1[:, half:V], x1[1])
+
+        def product(bank, d, m, a, b):
+            if d == 0:
+                at = m * (P + V)
+                w_codes, w_scales = codes0[:, at : at + P], scales0[:, at : at + P]
+                x_codes, x_scales = codes0[:, P + a : P + b], scales0[:, P + a : P + b]
+            else:
+                w_codes, w_scales = w1_codes[:, m * P : (m + 1) * P], scales1[:, V + m * P : V + (m + 1) * P]
+                x_codes = x1a_codes[:, a:b] if a < half else x1b_codes[:, a - half : b - half]
+                x_scales = scales1[:, a:b]
+            nc.tensor.matmul_mx(
+                out=bank,
+                lhsT=w_codes.bitcast(FP8X4),
+                lhsT_scale=w_scales,
+                rhs=x_codes.bitcast(FP8X4),
+                rhs_scale=x_scales,
+                start=True,
+                stop=True,
+            )
 
         y0 = [keep.tile([P, V], F32, name=f"y0_{m}") for m in range(2)]
         for place, (m, cuts) in enumerate(((0, (0, 256)), (0, (256, 384, 512)), (1, (0, 256)), (1, (256, 512)))):
@@ -121,10 +117,10 @@ def tile_picked_pair_lin_mul_sub_e_kernel(tc, xT, w, offs, out):
                 product(bank[:, a - cuts[0] : b - cuts[0]], 0, m, a, b)
             nc.scalar.copy(out=y0[m][:, cuts[0] : cuts[-1]], in_=bank[:])
         result = [keep.tile([P, V], F32, name=f"result{m}") for m in range(2)]
-        pieces = ((0, 0, 128, 0), (0, 128, 256, 4), (0, 256, 384, 1), (0, 384, 512, 5), (1, 0, 256, 2), (1, 256, 512, 3))
-        for m, a, b, place in pieces:
-            bank = psum.tile([P, 256], F32, name=f"y1_bank{place}", tag=f"bank{place}")
-            product(bank[:, 0 : b - a], 1, m, a, b)
-            nc.vector.tensor_tensor(result[m][:, a:b], bank[:, 0 : b - a], y0[m][:, a:b], MULT)
-        for m, a, b in ((0, 0, 128), (0, 128, 256), (0, 256, 512), (1, 0, 256), (1, 256, 512)):
+        pieces = [(m, h * half + q * P) for h in range(2) for m in range(2) for q in range(2)]
+        for place, (m, a) in enumerate(pieces):
+            bank = psum.tile([P, 256], F32, name=f"y1_bank{place}", tag=f"bank{(place + 4) % 8}")
+            product(bank[:, 0:P], 1, m, a, a + P)
+            nc.vector.tensor_tensor(result[m][:, a : a + P], bank[:, 0:P], y0[m][:, a : a + P], MULT)
+        for m, a, b in ((0, 0, 128), (0, 128, 256), (1, 0, 256), (0, 256, 512), (1, 256, 512)):
             nc.sync.dma_start(out=out[m * P : (m + 1) * P, a:b], in_=result[m][:, a:b])

@@ -28,29 +28,28 @@ def tile_picked_pair_lin_mul_sub_e_kernel(tc, xT, w, offs, out):
         def entries(a, b):
             return offsets[:, a // 16 : b // 16]
 
-        last = PACK - 1
         half = V // 2
-        middle = keep.tile([P, 2, T], F32, name="middle")
-        first_plane = keep.tile([P, T], F32, name="first_plane")
-        last_plane = keep.tile([P, T], F32, name="last_plane")
+        early = keep.tile([P, 2, T], F32, name="early")
+        late = [keep.tile([P, T], F32, name=f"late{j}") for j in range(2)]
         w_raw = [keep.tile([P, PACK, N], F32, name=f"w_raw{d}", tag=f"shared{d}", align_bytes=64) for d in range(2)]
         x_rows = xT.rearrange("(p j) t -> p j t", j=PACK)
-        nc.sync.dma_start(out=middle[:], in_=x_rows[:, 1:last, :])
+        nc.sync.dma_start(out=early[:], in_=x_rows[:, 0:2, :])
         nc.sync.dma_start(offsets[:], offs)
-        nc.sync.dma_start(out=first_plane[:], in_=x_rows[:, 0, :])
-        nc.sync.dma_start(out=last_plane[:], in_=x_rows[:, last, :])
+        for j in range(2):
+            nc.sync.dma_start(out=late[j][:], in_=x_rows[:, 2 + j, :])
         for d in range(2):
             nc.sync.dma_start(out=w_raw[d][:], in_=w[d].rearrange("(p j) n -> p j n", j=PACK))
 
-        tile0 = keep.tile([P, V + N, PACK], BF16, name="tile0", align_bytes=64)
-        tile1 = keep.tile([P, V + N + P, PACK], BF16, name="tile1", align_bytes=64)
-        flat1 = tile1[:].rearrange("p c j -> p (c j)")
-        w_in = ((tile0[:, 0:P, :], tile0[:, P + V :, :]), (tile1[:, 352:480, :], tile1[:, 768:, :]))
-        x0 = tile0[:, P : P + V, :]
-        x1 = [tile1[:, 96:352, :], tile1[:, 512:768, :]]
+        first = keep.tile([P, V + N, PACK], BF16, name="first", align_bytes=64)
+        second = keep.tile([P, V + N, PACK], BF16, name="second", align_bytes=64)
+        w_in = ((first[:, 0:P, :], first[:, P + V :, :]), (second[:, V : V + P, :], second[:, V + P :, :]))
+        x_in = (first[:, P : P + V, :], second[:, 0:V, :])
 
-        def interleave_w(d, m):
-            nc.scalar.copy(
+        def picked(a, b, j):
+            return x_in[a // V][:, a % V : a % V + b - a, j]
+
+        def interleave_w(copy, d, m):
+            copy(
                 out=w_in[d][m].rearrange("p (c i) j -> p c j i", i=RUN),
                 in_=w_raw[d][:, :, m * P : (m + 1) * P].rearrange("p j (c i) -> p c j i", i=RUN),
             )
@@ -58,38 +57,39 @@ def tile_picked_pair_lin_mul_sub_e_kernel(tc, xT, w, offs, out):
         def quantise(codes, scales, values):
             nc.vector.quantize_mx(out=codes.bitcast(FP8X4), scales=scales, in_=values.rearrange("p c j -> p (c j)"))
 
-        dense = keep.tile([P, last, V], F32, name="dense")
-        for j in (1, 2, 0):
-            window = middle[:, j - 1, :] if j else first_plane[:]
-            nc.vector.tensor_copy(x0[:, :, j], window.indirect(entries(0, V)))
-            nc.scalar.activation(dense[:, j, :], window.indirect(entries(V, S)), COPY)
-        for h in range(2):
-            nc.vector.tensor_copy(
-                out=x1[h][:, :, 0:last], in_=dense[:, :, h * half : (h + 1) * half].rearrange("p j c -> p c j")
-            )
+        dense = keep.tile([P, 2, V], F32, name="dense")
+        for j in range(2):
+            nc.vector.tensor_copy(picked(0, V, j), early[:, j, :].indirect(entries(0, V)))
+            nc.scalar.activation(dense[:, j, :], early[:, j, :].indirect(entries(V, S)), COPY)
+        nc.vector.tensor_copy(out=x_in[1][:, :, 0:2], in_=dense[:].rearrange("p j c -> p c j"))
 
-        nc.vector.tensor_copy(x0[:, :, last], last_plane[:].indirect(entries(0, V)))
-        nc.scalar.activation(flat1[:, 0:384], last_plane[:].indirect(entries(V, V + 384)), COPY)
-        nc.scalar.activation(flat1[:, 1920:2048], last_plane[:].indirect(entries(V + 384, S)), COPY)
-        nc.vector.tensor_copy(out=x1[0][:, :, last], in_=flat1[:, 0:half])
-        interleave_w(0, 0)
-        interleave_w(0, 1)
+        staged = keep.tile([P, 2, P], BF16, name="staged")
+        for j in range(2):
+            nc.vector.tensor_copy(staged[:, j, :], late[j][:].indirect(entries(0, P)))
+            nc.vector.tensor_copy(out=picked(0, P, 2 + j), in_=staged[:, j, :])
+            for a, b in ((P, half), (half, V), (V, V + half), (V + half, S)):
+                nc.scalar.activation(picked(a, b, 2 + j), late[j][:].indirect(entries(a, b)), COPY)
+
         codes0 = keep.tile([P, V + N], U32, name="codes0", align_bytes=64)
         scales0 = keep.tile([P, V + N], U8, name="scales0", align_bytes=64)
-        quantise(codes0[:, 0:512], scales0[:, 0:512], tile0[:, 0:512, :])
-        quantise(codes0[:, 512:], scales0[:, 512:], tile0[:, 512:, :])
         scales1 = keep.tile([P, V + N], U8, name="scales1", align_bytes=64)
         w1_codes = keep.tile([P, N], U32, name="w1_codes", align_bytes=64)
-        x1a_codes = keep.tile([P, half], U32, name="x1a_codes", tag="shared0", align_bytes=64)
-        quantise(x1a_codes[:], scales1[:, 0:half], x1[0])
-        interleave_w(1, 0)
-        quantise(w1_codes[:, 0:P], scales1[:, V : V + P], w_in[1][0])
-        staged = flat1[:, half:2048].rearrange("p (g c) -> p g c", c=P)
-        nc.vector.tensor_copy(out=x1[1][:, :, last].rearrange("p (g c) -> p g c", c=P), in_=staged[:, 0::13, :])
-        interleave_w(1, 1)
-        quantise(w1_codes[:, P:], scales1[:, V + P :], w_in[1][1])
-        x1b_codes = keep.tile([P, half], U32, name="x1b_codes", tag="shared1", align_bytes=64)
-        quantise(x1b_codes[:], scales1[:, half:V], x1[1])
+
+        def quantise_first(a, b):
+            quantise(codes0[:, a:b], scales0[:, a:b], first[:, a:b, :])
+
+        quantise_first(2 * P, 3 * P)
+        interleave_w(nc.vector.tensor_copy, 0, 0)
+        interleave_w(nc.vector.tensor_copy, 0, 1)
+        quantise_first(0, 2 * P)
+        quantise_first(3 * P, V + N)
+        x1_codes = keep.tile([P, V], U32, name="x1_codes", tag="shared0", align_bytes=64)
+        interleave_w(nc.vector.tensor_copy, 1, 0)
+        interleave_w(nc.scalar.copy, 1, 1)
+        for h in range(2):
+            cols = slice(h * half, (h + 1) * half)
+            quantise(x1_codes[:, cols], scales1[:, cols], x_in[1][:, cols, :])
+            quantise(w1_codes[:, h * P : (h + 1) * P], scales1[:, V + h * P : V + (h + 1) * P], w_in[1][h])
 
         def product(bank, d, m, a, b):
             if d == 0:
@@ -98,8 +98,7 @@ def tile_picked_pair_lin_mul_sub_e_kernel(tc, xT, w, offs, out):
                 x_codes, x_scales = codes0[:, P + a : P + b], scales0[:, P + a : P + b]
             else:
                 w_codes, w_scales = w1_codes[:, m * P : (m + 1) * P], scales1[:, V + m * P : V + (m + 1) * P]
-                x_codes = x1a_codes[:, a:b] if a < half else x1b_codes[:, a - half : b - half]
-                x_scales = scales1[:, a:b]
+                x_codes, x_scales = x1_codes[:, a:b], scales1[:, a:b]
             nc.tensor.matmul_mx(
                 out=bank,
                 lhsT=w_codes.bitcast(FP8X4),
@@ -111,16 +110,16 @@ def tile_picked_pair_lin_mul_sub_e_kernel(tc, xT, w, offs, out):
             )
 
         y0 = [keep.tile([P, V], F32, name=f"y0_{m}") for m in range(2)]
-        for place, (m, cuts) in enumerate(((0, (0, 256)), (0, (256, 384, 512)), (1, (0, 256)), (1, (256, 512)))):
-            bank = psum.tile([P, 256], F32, name=f"y0_bank{place}", tag=f"bank{place}")
-            for a, b in zip(cuts, cuts[1:]):
-                product(bank[:, a - cuts[0] : b - cuts[0]], 0, m, a, b)
-            nc.scalar.copy(out=y0[m][:, cuts[0] : cuts[-1]], in_=bank[:])
+        for place, (m, a, b) in enumerate(((0, 0, half), (0, half, V), (1, 0, V))):
+            bank = psum.tile([P, V], F32, name=f"y0_bank{place}", tag=f"bank{place}")
+            product(bank[:, 0 : b - a], 0, m, a, b)
+            for c in range(a, b, half):
+                nc.scalar.copy(out=y0[m][:, c : c + half], in_=bank[:, c - a : c - a + half])
         result = [keep.tile([P, V], F32, name=f"result{m}") for m in range(2)]
-        pieces = [(m, h * half + q * P) for h in range(2) for m in range(2) for q in range(2)]
+        pieces = [(m, a) for m in range(2) for a in range(0, V, P)]
         for place, (m, a) in enumerate(pieces):
-            bank = psum.tile([P, 256], F32, name=f"y1_bank{place}", tag=f"bank{(place + 4) % 8}")
+            bank = psum.tile([P, V], F32, name=f"y1_bank{place}", tag=f"bank{(3, 4, 5, 6, 7, 0, 1, 3)[place]}")
             product(bank[:, 0:P], 1, m, a, a + P)
             nc.vector.tensor_tensor(result[m][:, a : a + P], bank[:, 0:P], y0[m][:, a : a + P], MULT)
-        for m, a, b in ((0, 0, 128), (0, 128, 256), (1, 0, 256), (0, 256, 512), (1, 256, 512)):
+        for m, a, b in ((0, 0, 128), (0, 128, 256), (0, 256, 512), (1, 0, 256), (1, 256, 512)):
             nc.sync.dma_start(out=out[m * P : (m + 1) * P, a:b], in_=result[m][:, a:b])

@@ -48,10 +48,10 @@ def tile_picked_pair_lin_mul_sub_e_kernel(tc, xT, w, offs, out):
         def picked(a, b, j):
             return x_in[a // V][:, a % V : a % V + b - a, j]
 
-        def interleave_w(copy, d, m):
+        def interleave_w(copy, d, m, a=0, b=P):
             copy(
-                out=w_in[d][m].rearrange("p (c i) j -> p c j i", i=RUN),
-                in_=w_raw[d][:, :, m * P : (m + 1) * P].rearrange("p j (c i) -> p c j i", i=RUN),
+                out=w_in[d][m][:, a:b, :].rearrange("p (c i) j -> p c j i", i=RUN),
+                in_=w_raw[d][:, :, m * P + a : m * P + b].rearrange("p j (c i) -> p c j i", i=RUN),
             )
 
         def quantise(codes, scales, values):
@@ -85,9 +85,11 @@ def tile_picked_pair_lin_mul_sub_e_kernel(tc, xT, w, offs, out):
         quantise_first(3 * P, V + N)
         x1_codes = keep.tile([P, V], U32, name="x1_codes", tag="shared0", align_bytes=64)
         interleave_w(nc.vector.tensor_copy, 1, 0)
-        interleave_w(nc.scalar.copy, 1, 1)
+        interleave_w(nc.scalar.copy, 1, 1, 0, P // 2)
         for h in range(2):
             cols = slice(h * half, (h + 1) * half)
+            if h == 1:
+                interleave_w(nc.vector.tensor_copy, 1, 1, P // 2, P)
             quantise(x1_codes[:, cols], scales1[:, cols], x_in[1][:, cols, :])
             quantise(w1_codes[:, h * P : (h + 1) * P], scales1[:, V + h * P : V + (h + 1) * P], w_in[1][h])
 

@@ -67,7 +67,7 @@ def tile_picked_pair_lin_mul_sub_e_kernel(tc, xT, w, offs, out):
         for j in range(2):
             nc.vector.tensor_copy(staged[:, j, :], late[j][:].indirect(entries(0, P)))
             nc.vector.tensor_copy(out=picked(0, P, 2 + j), in_=staged[:, j, :])
-            for a, b in ((P, half), (half, V), (V, V + half), (V + half, S)):
+            for a, b in ((P, half), (half, V), (V, V + half), (V + half, S - P), (S - P, S)):
                 nc.scalar.activation(picked(a, b, 2 + j), late[j][:].indirect(entries(a, b)), COPY)
 
         codes0 = keep.tile([P, V + N], U32, name="codes0", align_bytes=64)
@@ -85,13 +85,20 @@ def tile_picked_pair_lin_mul_sub_e_kernel(tc, xT, w, offs, out):
         quantise_first(3 * P, V + N)
         x1_codes = keep.tile([P, V], U32, name="x1_codes", tag="shared0", align_bytes=64)
         interleave_w(nc.vector.tensor_copy, 1, 0)
-        interleave_w(nc.scalar.copy, 1, 1, 0, P // 2)
-        for h in range(2):
-            cols = slice(h * half, (h + 1) * half)
-            if h == 1:
-                interleave_w(nc.vector.tensor_copy, 1, 1, P // 2, P)
-            quantise(x1_codes[:, cols], scales1[:, cols], x_in[1][:, cols, :])
-            quantise(w1_codes[:, h * P : (h + 1) * P], scales1[:, V + h * P : V + (h + 1) * P], w_in[1][h])
+        interleave_w(nc.scalar.copy, 1, 1, 0, P - 96)
+
+        def quantise_x1(a, b):
+            quantise(x1_codes[:, a:b], scales1[:, a:b], x_in[1][:, a:b, :])
+
+        def quantise_w1(m):
+            quantise(w1_codes[:, m * P : (m + 1) * P], scales1[:, V + m * P : V + (m + 1) * P], w_in[1][m])
+
+        quantise_x1(0, half)
+        quantise_w1(0)
+        interleave_w(nc.vector.tensor_copy, 1, 1, P - 96, P)
+        quantise_x1(half, V - P)
+        quantise_x1(V - P, V)
+        quantise_w1(1)
 
         def product(bank, d, m, a, b):
             if d == 0:

@@ -3,7 +3,7 @@ import concourse.mybir as mybir
 K, T, S, V, N = 512, 4096, 1024, 512, 256
 P = 128
 PACK = 4
-RUN = 4
+RUN = 2
 
 FLOPS = 2 * K * N * S
 

@@ -3,7 +3,11 @@ import concourse.mybir as mybir
 K, T, S, V, N = 512, 4096, 1024, 512, 256
 P = 128
 PACK = 4
-RUN = 2
+HALF = V // 2
+OFFSETS_PER_COLUMN = 16
+RUN = 8
+SCALAR_SHARE = 32
+BANKS = 8
 
 FLOPS = 2 * K * N * S
 
@@ -23,12 +27,11 @@ def tile_picked_pair_lin_mul_sub_e_kernel(tc, xT, w, offs, out):
         tc.tile_pool(name="keep", bufs=1) as keep,
         tc.psum_pool(name="psum", bufs=1) as psum,
     ):
-        offsets = keep.tile([P, S // 16], U16, name="offsets")
+        offsets = keep.tile([P, S // OFFSETS_PER_COLUMN], U16, name="offsets")
 
         def entries(a, b):
-            return offsets[:, a // 16 : b // 16]
+            return offsets[:, a // OFFSETS_PER_COLUMN : b // OFFSETS_PER_COLUMN]
 
-        half = V // 2
         early = keep.tile([P, 2, T], F32, name="early")
         late = [keep.tile([P, T], F32, name=f"late{j}") for j in range(2)]
         w_raw = [keep.tile([P, PACK, N], F32, name=f"w_raw{d}", tag=f"shared{d}", align_bytes=64) for d in range(2)]
@@ -45,8 +48,8 @@ def tile_picked_pair_lin_mul_sub_e_kernel(tc, xT, w, offs, out):
         w_in = ((first[:, 0:P, :], first[:, P + V :, :]), (second[:, V : V + P, :], second[:, V + P :, :]))
         x_in = (first[:, P : P + V, :], second[:, 0:V, :])
 
-        def picked(a, b, j):
-            return x_in[a // V][:, a % V : a % V + b - a, j]
+        def picked(a, b, slot):
+            return x_in[a // V][:, a % V : a % V + b - a, slot]
 
         def interleave_w(copy, d, m, a=0, b=P):
             copy(
@@ -64,10 +67,11 @@ def tile_picked_pair_lin_mul_sub_e_kernel(tc, xT, w, offs, out):
         nc.vector.tensor_copy(out=x_in[1][:, :, 0:2], in_=dense[:].rearrange("p j c -> p c j"))
 
         staged = keep.tile([P, 2, P], BF16, name="staged")
+        scalar_cuts = (P, HALF, V, V + HALF, S - P, S)
         for j in range(2):
             nc.vector.tensor_copy(staged[:, j, :], late[j][:].indirect(entries(0, P)))
             nc.vector.tensor_copy(out=picked(0, P, 2 + j), in_=staged[:, j, :])
-            for a, b in ((P, half), (half, V), (V, V + half), (V + half, S - P), (S - P, S)):
+            for a, b in zip(scalar_cuts, scalar_cuts[1:]):
                 nc.scalar.activation(picked(a, b, 2 + j), late[j][:].indirect(entries(a, b)), COPY)
 
         codes0 = keep.tile([P, V + N], U32, name="codes0", align_bytes=64)
@@ -83,9 +87,10 @@ def tile_picked_pair_lin_mul_sub_e_kernel(tc, xT, w, offs, out):
         interleave_w(nc.vector.tensor_copy, 0, 1)
         quantise_first(0, 2 * P)
         quantise_first(3 * P, V + N)
+
         x1_codes = keep.tile([P, V], U32, name="x1_codes", tag="shared0", align_bytes=64)
         interleave_w(nc.vector.tensor_copy, 1, 0)
-        interleave_w(nc.scalar.copy, 1, 1, 0, P - 96)
+        interleave_w(nc.scalar.copy, 1, 1, 0, SCALAR_SHARE)
 
         def quantise_x1(a, b):
             quantise(x1_codes[:, a:b], scales1[:, a:b], x_in[1][:, a:b, :])
@@ -93,10 +98,10 @@ def tile_picked_pair_lin_mul_sub_e_kernel(tc, xT, w, offs, out):
         def quantise_w1(m):
             quantise(w1_codes[:, m * P : (m + 1) * P], scales1[:, V + m * P : V + (m + 1) * P], w_in[1][m])
 
-        quantise_x1(0, half)
+        quantise_x1(0, HALF)
         quantise_w1(0)
-        interleave_w(nc.vector.tensor_copy, 1, 1, P - 96, P)
-        quantise_x1(half, V - P)
+        interleave_w(nc.vector.tensor_copy, 1, 1, SCALAR_SHARE, P)
+        quantise_x1(HALF, V - P)
         quantise_x1(V - P, V)
         quantise_w1(1)
 
@@ -118,17 +123,22 @@ def tile_picked_pair_lin_mul_sub_e_kernel(tc, xT, w, offs, out):
                 stop=True,
             )
 
+        y0_passes = ((0, 0, HALF), (0, HALF, V), (1, 0, V))
         y0 = [keep.tile([P, V], F32, name=f"y0_{m}") for m in range(2)]
-        for place, (m, a, b) in enumerate(((0, 0, half), (0, half, V), (1, 0, V))):
+        for place, (m, a, b) in enumerate(y0_passes):
             bank = psum.tile([P, V], F32, name=f"y0_bank{place}", tag=f"bank{place}")
             product(bank[:, 0 : b - a], 0, m, a, b)
-            for c in range(a, b, half):
-                nc.scalar.copy(out=y0[m][:, c : c + half], in_=bank[:, c - a : c - a + half])
+            for c in range(a, b, HALF):
+                nc.scalar.copy(out=y0[m][:, c : c + HALF], in_=bank[:, c - a : c - a + HALF])
+
+        unused = list(range(len(y0_passes), BANKS))
+        y1_banks = unused + [0, 1] + unused[:1]
         result = [keep.tile([P, V], F32, name=f"result{m}") for m in range(2)]
         pieces = [(m, a) for m in range(2) for a in range(0, V, P)]
         for place, (m, a) in enumerate(pieces):
-            bank = psum.tile([P, V], F32, name=f"y1_bank{place}", tag=f"bank{(3, 4, 5, 6, 7, 0, 1, 3)[place]}")
+            bank = psum.tile([P, V], F32, name=f"y1_bank{place}", tag=f"bank{y1_banks[place]}")
             product(bank[:, 0:P], 1, m, a, a + P)
             nc.vector.tensor_tensor(result[m][:, a : a + P], bank[:, 0:P], y0[m][:, a : a + P], MULT)
-        for m, a, b in ((0, 0, 128), (0, 128, 256), (0, 256, 512), (1, 0, 256), (1, 256, 512)):
+
+        for m, a, b in ((0, 0, P), (0, P, HALF), (0, HALF, V), (1, 0, HALF), (1, HALF, V)):
             nc.sync.dma_start(out=out[m * P : (m + 1) * P, a:b], in_=result[m][:, a:b])

import concourse.mybir as mybir

K, T, S, V, N = 512, 4096, 1024, 512, 256
P = 128
PACK = 4
HALF = V // 2
OFFSETS_PER_COLUMN = 16
RUN = 8
SCALAR_SHARE = 32
BANKS = 8

FLOPS = 2 * K * N * S

F32 = mybir.dt.float32
BF16 = mybir.dt.bfloat16
U32 = mybir.dt.uint32
U16 = mybir.dt.uint16
U8 = mybir.dt.uint8
FP8X4 = mybir.dt.float8_e4m3fn_x4
MULT = mybir.AluOpType.mult
COPY = mybir.ActivationFunctionType.Copy


def tile_picked_pair_lin_mul_sub_e_kernel(tc, xT, w, offs, out):
    nc = tc.nc
    with (
        tc.tile_pool(name="keep", bufs=1) as keep,
        tc.psum_pool(name="psum", bufs=1) as psum,
    ):
        offsets = keep.tile([P, S // OFFSETS_PER_COLUMN], U16, name="offsets")

        def entries(a, b):
            return offsets[:, a // OFFSETS_PER_COLUMN : b // OFFSETS_PER_COLUMN]

        early = keep.tile([P, 2, T], F32, name="early")
        late = [keep.tile([P, T], F32, name=f"late{j}") for j in range(2)]
        w_raw = [keep.tile([P, PACK, N], F32, name=f"w_raw{d}", tag=f"shared{d}", align_bytes=64) for d in range(2)]
        x_rows = xT.rearrange("(p j) t -> p j t", j=PACK)
        nc.sync.dma_start(out=early[:], in_=x_rows[:, 0:2, :])
        nc.sync.dma_start(offsets[:], offs)
        for j in range(2):
            nc.sync.dma_start(out=late[j][:], in_=x_rows[:, 2 + j, :])
        for d in range(2):
            nc.sync.dma_start(out=w_raw[d][:], in_=w[d].rearrange("(p j) n -> p j n", j=PACK))

        first = keep.tile([P, V + N, PACK], BF16, name="first", align_bytes=64)
        second = keep.tile([P, V + N, PACK], BF16, name="second", align_bytes=64)
        w_in = ((first[:, 0:P, :], first[:, P + V :, :]), (second[:, V : V + P, :], second[:, V + P :, :]))
        x_in = (first[:, P : P + V, :], second[:, 0:V, :])

        def picked(a, b, slot):
            return x_in[a // V][:, a % V : a % V + b - a, slot]

        def interleave_w(copy, d, m, a=0, b=P):
            copy(
                out=w_in[d][m][:, a:b, :].rearrange("p (c i) j -> p c j i", i=RUN),
                in_=w_raw[d][:, :, m * P + a : m * P + b].rearrange("p j (c i) -> p c j i", i=RUN),
            )

        def quantise(codes, scales, values):
            nc.vector.quantize_mx(out=codes.bitcast(FP8X4), scales=scales, in_=values.rearrange("p c j -> p (c j)"))

        dense = keep.tile([P, 2, V], F32, name="dense")
        for j in range(2):
            nc.vector.tensor_copy(picked(0, V, j), early[:, j, :].indirect(entries(0, V)))
            nc.scalar.activation(dense[:, j, :], early[:, j, :].indirect(entries(V, S)), COPY)
        nc.vector.tensor_copy(out=x_in[1][:, :, 0:2], in_=dense[:].rearrange("p j c -> p c j"))

        staged = keep.tile([P, 2, P], BF16, name="staged")
        scalar_cuts = (P, HALF, V, V + HALF, S - P, S)
        for j in range(2):
            nc.vector.tensor_copy(staged[:, j, :], late[j][:].indirect(entries(0, P)))
            nc.vector.tensor_copy(out=picked(0, P, 2 + j), in_=staged[:, j, :])
            for a, b in zip(scalar_cuts, scalar_cuts[1:]):
                nc.scalar.activation(picked(a, b, 2 + j), late[j][:].indirect(entries(a, b)), COPY)

        codes0 = keep.tile([P, V + N], U32, name="codes0", align_bytes=64)
        scales0 = keep.tile([P, V + N], U8, name="scales0", align_bytes=64)
        scales1 = keep.tile([P, V + N], U8, name="scales1", align_bytes=64)
        w1_codes = keep.tile([P, N], U32, name="w1_codes", align_bytes=64)

        def quantise_first(a, b):
            quantise(codes0[:, a:b], scales0[:, a:b], first[:, a:b, :])

        quantise_first(2 * P, 3 * P)
        interleave_w(nc.vector.tensor_copy, 0, 0)
        interleave_w(nc.vector.tensor_copy, 0, 1)
        quantise_first(0, 2 * P)
        quantise_first(3 * P, V + N)

        x1_codes = keep.tile([P, V], U32, name="x1_codes", tag="shared0", align_bytes=64)
        interleave_w(nc.vector.tensor_copy, 1, 0)
        interleave_w(nc.scalar.copy, 1, 1, 0, SCALAR_SHARE)

        def quantise_x1(a, b):
            quantise(x1_codes[:, a:b], scales1[:, a:b], x_in[1][:, a:b, :])

        def quantise_w1(m):
            quantise(w1_codes[:, m * P : (m + 1) * P], scales1[:, V + m * P : V + (m + 1) * P], w_in[1][m])

        quantise_x1(0, HALF)
        quantise_w1(0)
        interleave_w(nc.vector.tensor_copy, 1, 1, SCALAR_SHARE, P)
        quantise_x1(HALF, V - P)
        quantise_x1(V - P, V)
        quantise_w1(1)

        def product(bank, d, m, a, b):
            if d == 0:
                at = m * (P + V)
                w_codes, w_scales = codes0[:, at : at + P], scales0[:, at : at + P]
                x_codes, x_scales = codes0[:, P + a : P + b], scales0[:, P + a : P + b]
            else:
                w_codes, w_scales = w1_codes[:, m * P : (m + 1) * P], scales1[:, V + m * P : V + (m + 1) * P]
                x_codes, x_scales = x1_codes[:, a:b], scales1[:, a:b]
            nc.tensor.matmul_mx(
                out=bank,
                lhsT=w_codes.bitcast(FP8X4),
                lhsT_scale=w_scales,
                rhs=x_codes.bitcast(FP8X4),
                rhs_scale=x_scales,
                start=True,
                stop=True,
            )

        y0_passes = ((0, 0, HALF), (0, HALF, V), (1, 0, V))
        y0 = [keep.tile([P, V], F32, name=f"y0_{m}") for m in range(2)]
        for place, (m, a, b) in enumerate(y0_passes):
            bank = psum.tile([P, V], F32, name=f"y0_bank{place}", tag=f"bank{place}")
            product(bank[:, 0 : b - a], 0, m, a, b)
            for c in range(a, b, HALF):
                nc.scalar.copy(out=y0[m][:, c : c + HALF], in_=bank[:, c - a : c - a + HALF])

        unused = list(range(len(y0_passes), BANKS))
        y1_banks = unused + [0, 1] + unused[:1]
        result = [keep.tile([P, V], F32, name=f"result{m}") for m in range(2)]
        pieces = [(m, a) for m in range(2) for a in range(0, V, P)]
        for place, (m, a) in enumerate(pieces):
            bank = psum.tile([P, V], F32, name=f"y1_bank{place}", tag=f"bank{y1_banks[place]}")
            product(bank[:, 0:P], 1, m, a, a + P)
            nc.vector.tensor_tensor(result[m][:, a : a + P], bank[:, 0:P], y0[m][:, a : a + P], MULT)

        for m, a, b in ((0, 0, P), (0, P, HALF), (0, HALF, V), (1, 0, HALF), (1, HALF, V)):
            nc.sync.dma_start(out=out[m * P : (m + 1) * P, a:b], in_=result[m][:, a:b])
